import numpy as np
import ml_dtypes


def mxq(x, axis, fmt="e4m3"):
    dtype, down = {"e4m3": (ml_dtypes.float8_e4m3fn, 7), "e5m2": (ml_dtypes.float8_e5m2, 14)}[fmt]
    v = np.moveaxis(np.asarray(x, np.float32).astype(ml_dtypes.bfloat16).astype(np.float64), axis, -1)
    blocks = v.reshape(v.shape[:-1] + (-1, 32))
    amax = np.abs(blocks).max(-1, keepdims=True)
    byte = np.maximum(np.where(amax > 0, np.frexp(amax)[1] - 1 + 127, 0) - down, 1)
    scale = np.exp2(byte - 127.0)
    codes = (blocks / scale).astype(np.float32).astype(dtype).astype(np.float64)
    return np.moveaxis((codes * scale).reshape(v.shape), -1, axis)


WIDE = False


def mx_kscale(k):
    if not WIDE:
        return np.ones(k)
    levels = np.array([10, -10, 5, -5, 0])
    if k % 512:
        return np.exp2(np.random.permutation(np.resize(levels, k // 32))).repeat(32)
    a = np.empty((k // 512, 16))
    for p in range(k // 512):
        a[p, :8] = np.random.permutation(np.resize(levels, 8))
        for g in range(8):
            far = levels[np.abs(levels - a[p, g]) >= 10]
            a[p, g + 8] = far[np.random.randint(len(far))]
    return np.exp2(a.ravel()).repeat(32)


def f64(x):
    return np.asarray(x).astype(np.float64)


def striped8(idx):
    return np.concatenate([x.reshape(-1, 16).T for x in idx]).astype(np.uint16)


def runs(offs, k):
    lists = np.stack([offs[16 * r : 16 * r + 16].T.reshape(-1) for r in range(8)]).astype(np.int64)
    return lists[np.arange(k) % 512 // 64]


def pack_weight(w):
    k, n = w.shape
    w = f64(np.asarray(w, np.float32).astype(ml_dtypes.bfloat16)).reshape(k // 32, 32, n)
    amax = np.abs(w).max(1)
    byte = np.clip(np.where(amax > 0, np.frexp(amax)[1] - 1 + 127 - 7, 1), 1, 254)
    scaled = (w * np.exp2(127.0 - byte)[:, None, :]).reshape(k, n).astype(np.float32)
    words = np.ascontiguousarray(scaled.reshape(k // 512, 128, 4, n).transpose(0, 1, 3, 2)).astype(ml_dtypes.float8_e4m3fn).view(np.uint8)
    return words, np.ascontiguousarray(byte.astype(np.uint8).reshape(k // 512, 16, n))


def unpack_weight(words, scales):
    g, p, n, _ = words.shape
    vals = np.ascontiguousarray(words).view(ml_dtypes.float8_e4m3fn).astype(np.float64) * np.repeat(np.exp2(scales.astype(np.float64) - 127.0), 8, axis=1)[..., None]
    return vals.transpose(0, 1, 3, 2).reshape(g * 512, n)


def gelu(v):
    return 0.5 * v * (1.0 + np.tanh(np.sqrt(2.0 / np.pi) * (v + 0.044715 * v**3)))


K, T, S, H, N, V = 512, 2048, 1024, 512, 128, 512


def setup_inputs():
    n = np.random.standard_normal
    s = mx_kscale(K)[:, None]
    u = mx_kscale(H)
    packed_xT = pack_weight(n((K, T)) * s)
    packed_w2 = pack_weight(n((H, N)) / np.sqrt(H) / u[:, None])
    return {
        "x_words": packed_xT[0],
        "x_scales": packed_xT[1],
        "w1": (n((K, H)) / np.sqrt(K) / s * u).astype(np.float32),
        "w2_words": packed_w2[0],
        "w2_scales": packed_w2[1],
        "offs": striped8(np.stack([np.random.permutation(T)[:S] for _ in range(8)])),
    }


def reference(x_words, x_scales, w1, w2_words, w2_scales, offs):
    xq = unpack_weight(x_words, x_scales)[np.arange(K)[:, None], runs(offs, K)]
    y = mxq(f64(w1), 0, "e4m3").T @ xq
    z = np.maximum(y[:, :V], y[:, V:2 * V])
    za = gelu(z)
    return unpack_weight(w2_words, w2_scales).T @ mxq(za, 0, "e4m3")

@@ -1,0 +1,141 @@
+from contextlib import ExitStack
+
+import concourse.mybir as mybir
+
+K, T, S, H, N, V = 512, 2048, 1024, 512, 128, 512
+FLOPS = 2 * K * H * S + 2 * H * N * V
+
+F32 = mybir.dt.float32
+BF16 = mybir.dt.bfloat16
+I32 = mybir.dt.int32
+U32 = mybir.dt.uint32
+U16 = mybir.dt.uint16
+U8 = mybir.dt.uint8
+FP8X4 = mybir.dt.float8_e4m3fn_x4
+GELU = mybir.ActivationFunctionType.Gelu_apprx_tanh
+MAX = mybir.AluOpType.max
+AX = mybir.AxisListType.X
+
+P = 128
+PACK = 4
+CH = 128
+NCH = V // CH
+REDUCE_CHUNKS = (3,)
+WARM = True
+OUT_ON_SCALAR = ()
+
+
+def tile_picked_phpool_gelu_p_kernel(tc, x_words, x_scales, w1, w2_words, w2_scales, offs, out):
+    nc = tc.nc
+    with ExitStack() as ctx:
+        keep = ctx.enter_context(tc.tile_pool(name="keep", bufs=1))
+        shared = ctx.enter_context(tc.tile_pool(name="shared", bufs=1))
+        work = ctx.enter_context(tc.tile_pool(name="work", bufs=4))
+        ypsum = ctx.enter_context(tc.psum_pool(name="ypsum", bufs=6))
+        opsum = ctx.enter_context(tc.psum_pool(name="opsum", bufs=2))
+
+        lists = keep.tile([P, S // 16], U16, name="lists")
+        nc.sync.dma_start(lists[:], offs)
+
+        xw = keep.tile([P, T], U32, name="xw", align_bytes=64)
+        nc.scalar.dma_start(xw[:].bitcast(I32), x_words[0].rearrange("p n t -> p (n t)").bitcast(I32))
+        w1_raw = keep.tile([P, PACK, H], F32, name="w1_raw", align_bytes=64)
+        nc.scalar.dma_start(w1_raw[:], w1.rearrange("(p j) c -> p j c", j=PACK))
+
+        xs = shared.tile([P, T], U8, name="xs", align_bytes=64, offset=0)
+        nc.vector.memset(xs[:].bitcast(I32), 0)
+        nc.sync.dma_start(xs[:].bitcast(I32)[0:P:8, :], x_scales[0].bitcast(I32))
+
+        if WARM:
+            zero = keep.tile([P, 1], F32, name="zero")
+            nc.vector.memset(zero[:], 0.0)
+            warm = keep.tile([P, 1], F32, name="warm")
+            nc.scalar.activation(warm[:], zero[:], GELU)
+
+        xs_placed = keep.tile([P, S], U8, name="xs_placed", align_bytes=64)
+        nc.vector.memset(xs_placed[:].bitcast(I32), 0)
+        w2w = keep.tile([P, N], U32, name="w2w", align_bytes=64)
+        nc.sync.dma_start(w2w[:].bitcast(I32), w2_words[0].rearrange("p n t -> p (n t)").bitcast(I32))
+
+        xs_picked = keep.tile([P, S], U8, name="xs_picked", align_bytes=64)
+        nc.vector.tensor_copy(xs_picked[:], xs[:].indirect(lists[:]))
+        for j in range(4):
+            nc.sync.dma_start(xs_placed[:].bitcast(I32)[j:P:32, :], xs_picked[:].bitcast(I32)[8 * j : P : 32, :])
+        w2s = shared.tile([P, N], U8, name="w2s", align_bytes=64, offset=0)
+        nc.vector.memset(w2s[:].bitcast(I32), 0)
+        for q in range(4):
+            nc.sync.dma_start(w2s[:].bitcast(I32)[32 * q : 32 * q + 4, :], w2_scales[0].bitcast(I32)[4 * q : 4 * q + 4, :])
+        xw_picked = shared.tile([P, S], U32, name="xw_picked", align_bytes=64, offset=N)
+        nc.vector.tensor_copy(xw_picked[:], xw[:].indirect(lists[:]))
+
+        half = P // 2
+        w1_bf = [keep.tile([P, PACK, half, PACK], BF16, name="w1_bf%d" % h, align_bytes=64) for h in range(2)]
+        for h in range(2):
+            src = w1_raw[:, :, PACK * half * h : PACK * half * (h + 1)].rearrange("p j (m t) -> p m j t", t=PACK)
+            dst = w1_bf[h][:].rearrange("p t m j -> p m j t")
+            if h == 0:
+                nc.scalar.copy(dst, src)
+            else:
+                nc.vector.tensor_copy(dst, src)
+        w1c = [keep.tile([P, P], U32, name="w1c%d" % t, align_bytes=64) for t in range(PACK)]
+        w1s = [keep.tile([P, P], U8, name="w1s%d" % t, align_bytes=64) for t in range(PACK)]
+        for h in (1, 0):
+            for t in range(PACK):
+                cols = slice(half * h, half * (h + 1))
+                nc.vector.quantize_mx(out=w1c[t][:, cols].bitcast(FP8X4), scales=w1s[t][:, cols], in_=w1_bf[h][:, t].rearrange("p m j -> p (m j)"))
+
+        def first(dst, t, col):
+            nc.tensor.matmul_mx(out=dst, lhsT=w1c[t][:].bitcast(FP8X4), lhsT_scale=w1s[t][:],
+                                rhs=xw_picked[:, col : col + CH].bitcast(FP8X4), rhs_scale=xs_placed[:, col : col + CH], start=True, stop=True)
+
+        zmax = {}
+        zbf = {}
+
+        def products(c):
+            zm = work.tile([P, CH * PACK], F32, name="zm", align_bytes=64)
+            if c in REDUCE_CHUNKS:
+                for u in range(2):
+                    bank = ypsum.tile([P, 2, 2, CH], F32, name="bank")
+                    for e in range(2):
+                        for r in range(2):
+                            first(bank[:, r, e, :], 2 * u + e, V * r + CH * c)
+                    nc.vector.tensor_reduce(zm[:, 2 * CH * u : 2 * CH * (u + 1)].rearrange("p (v e) -> p v e", e=2),
+                                            bank[:].rearrange("p r e v -> p v e r"), AX, MAX)
+                zmax[c] = zm[:].rearrange("p (u v e) -> p v u e", u=2, e=2)
+            else:
+                bank_a = ypsum.tile([P, 2, 2, CH], F32, name="bank")
+                for t in range(PACK):
+                    first(bank_a[:, t // 2, t % 2, :], t, CH * c)
+                ya = work.tile([P, CH, PACK], F32, name="ya", align_bytes=64)
+                nc.scalar.copy(ya[:], bank_a[:].rearrange("p u e v -> p v (u e)"))
+                bank_b = ypsum.tile([P, 2, 2, CH], F32, name="bank")
+                for t in range(PACK):
+                    first(bank_b[:, t // 2, t % 2, :], t, V + CH * c)
+                nc.vector.tensor_tensor(zm[:].rearrange("p (v t) -> p v t", t=PACK), bank_b[:].rearrange("p u e v -> p v (u e)"), ya[:], MAX)
+                zmax[c] = zm[:].rearrange("p (v u e) -> p v u e", u=2, e=2)
+
+        def activate(c):
+            zb = work.tile([P, CH * PACK], BF16, name="zb", align_bytes=64)
+            nc.scalar.activation(zb[:].rearrange("p (v u e) -> p v u e", u=2, e=2), zmax[c], GELU)
+            zbf[c] = zb
+
+        def second(c):
+            zc = work.tile([P, CH], U32, name="zc", align_bytes=64)
+            zs = work.tile([P, CH], U8, name="zs", align_bytes=64)
+            nc.vector.quantize_mx(out=zc[:].bitcast(FP8X4), scales=zs[:], in_=zbf[c][:])
+            acc = opsum.tile([P, CH], F32, name="acc")
+            nc.tensor.matmul_mx(out=acc[:], lhsT=w2w[:].bitcast(FP8X4), lhsT_scale=w2s[:], rhs=zc[:].bitcast(FP8X4), rhs_scale=zs[:], start=True, stop=True)
+            res = work.tile([P, CH], F32, name="res", align_bytes=64)
+            if c in OUT_ON_SCALAR:
+                nc.scalar.copy(res[:], acc[:])
+            else:
+                nc.vector.tensor_copy(res[:], acc[:])
+            nc.sync.dma_start(out[:, CH * c : CH * (c + 1)], res[:])
+
+        for step in range(NCH + 2):
+            if step < NCH:
+                products(step)
+            if 0 <= step - 1 < NCH:
+                activate(step - 1)
+            if 0 <= step - 2 < NCH:
+                second(step - 2)

@@ -20,9 +20,14 @@ P = 128
 PACK = 4
 CH = 128
 NCH = V // CH
-REDUCE_CHUNKS = (3,)
+REDUCE_CHUNKS = ()
+PEWARM = 4
+GROUPS = ((0, 1), (2,), (3,))
+ORDER = "a0 a1 a2 b0 a3 b1 g0 b2 g1 b3 g2 q0 g3 q1 o0 q2 o1 o2"
+REPL = True
+GORDER = (0, 1, 2, 3)
 WARM = True
-OUT_ON_SCALAR = ()
+OUT_ON_SCALAR = (1, 2)
 
 
 def tile_picked_phpool_gelu_p_kernel(tc, x_words, x_scales, w1, w2_words, w2_scales, offs, out):
@@ -31,20 +36,25 @@ def tile_picked_phpool_gelu_p_kernel(tc, x_words, x_scales, w1, w2_words, w2_sca
         keep = ctx.enter_context(tc.tile_pool(name="keep", bufs=1))
         shared = ctx.enter_context(tc.tile_pool(name="shared", bufs=1))
         work = ctx.enter_context(tc.tile_pool(name="work", bufs=4))
-        ypsum = ctx.enter_context(tc.psum_pool(name="ypsum", bufs=6))
-        opsum = ctx.enter_context(tc.psum_pool(name="opsum", bufs=2))
+        ypsum = ctx.enter_context(tc.psum_pool(name="ypsum", bufs=5))
+        opsum = ctx.enter_context(tc.psum_pool(name="opsum", bufs=3))
 
         lists = keep.tile([P, S // 16], U16, name="lists")
         nc.sync.dma_start(lists[:], offs)
 
-        xw = keep.tile([P, T], U32, name="xw", align_bytes=64)
-        nc.scalar.dma_start(xw[:].bitcast(I32), x_words[0].rearrange("p n t -> p (n t)").bitcast(I32))
+        w1_rows = w1.rearrange("(p j) c -> p j c", j=PACK)
         w1_raw = keep.tile([P, PACK, H], F32, name="w1_raw", align_bytes=64)
-        nc.scalar.dma_start(w1_raw[:], w1.rearrange("(p j) c -> p j c", j=PACK))
-
         xs = shared.tile([P, T], U8, name="xs", align_bytes=64, offset=0)
-        nc.vector.memset(xs[:].bitcast(I32), 0)
-        nc.sync.dma_start(xs[:].bitcast(I32)[0:P:8, :], x_scales[0].bitcast(I32))
+        if REPL:
+            nc.sync.dma_start(xs[:].bitcast(I32), x_scales[0].bitcast(I32).unsqueeze(1).to_broadcast([16, 8, T // 4]))
+            nc.sync.dma_start(w1_raw[:], w1_rows)
+        else:
+            nc.sync.dma_start(w1_raw[:, 0:1], w1_rows[:, 0:1])
+            nc.vector.memset(xs[:].bitcast(I32), 0)
+            nc.sync.dma_start(xs[:].bitcast(I32)[0:P:8, :], x_scales[0].bitcast(I32))
+            nc.sync.dma_start(w1_raw[:, 1:PACK], w1_rows[:, 1:PACK])
+        xw = keep.tile([P, T], U32, name="xw", align_bytes=64)
+        nc.sync.dma_start(xw[:].bitcast(I32), x_words[0].rearrange("p n t -> p (n t)").bitcast(I32))
 
         if WARM:
             zero = keep.tile([P, 1], F32, name="zero")
@@ -65,77 +75,106 @@ def tile_picked_phpool_gelu_p_kernel(tc, x_words, x_scales, w1, w2_words, w2_sca
         nc.vector.memset(w2s[:].bitcast(I32), 0)
         for q in range(4):
             nc.sync.dma_start(w2s[:].bitcast(I32)[32 * q : 32 * q + 4, :], w2_scales[0].bitcast(I32)[4 * q : 4 * q + 4, :])
-        xw_picked = shared.tile([P, S], U32, name="xw_picked", align_bytes=64, offset=N)
-        nc.vector.tensor_copy(xw_picked[:], xw[:].indirect(lists[:]))
 
-        half = P // 2
-        w1_bf = [keep.tile([P, PACK, half, PACK], BF16, name="w1_bf%d" % h, align_bytes=64) for h in range(2)]
-        for h in range(2):
-            src = w1_raw[:, :, PACK * half * h : PACK * half * (h + 1)].rearrange("p j (m t) -> p m j t", t=PACK)
-            dst = w1_bf[h][:].rearrange("p t m j -> p m j t")
-            if h == 0:
+        w1_bf = [keep.tile([P, 2, P, PACK], BF16, name="w1_bf%d" % u, align_bytes=64) for u in range(2)]
+        w1c = keep.tile([P, H], U32, name="w1c", align_bytes=64)
+        w1s = keep.tile([P, H], U8, name="w1s", align_bytes=64)
+        for u in (1, 0):
+            src = w1_raw[:].rearrange("p j (m u e) -> p u m j e", u=2, e=2)[:, u]
+            dst = w1_bf[u][:].rearrange("p e m j -> p m j e")
+            if u == 1:
                 nc.scalar.copy(dst, src)
             else:
                 nc.vector.tensor_copy(dst, src)
-        w1c = [keep.tile([P, P], U32, name="w1c%d" % t, align_bytes=64) for t in range(PACK)]
-        w1s = [keep.tile([P, P], U8, name="w1s%d" % t, align_bytes=64) for t in range(PACK)]
-        for h in (1, 0):
-            for t in range(PACK):
-                cols = slice(half * h, half * (h + 1))
-                nc.vector.quantize_mx(out=w1c[t][:, cols].bitcast(FP8X4), scales=w1s[t][:, cols], in_=w1_bf[h][:, t].rearrange("p m j -> p (m j)"))
+        for u in (0, 1):
+            cols = slice(2 * P * u, 2 * P * (u + 1))
+            nc.vector.quantize_mx(out=w1c[:, cols].bitcast(FP8X4), scales=w1s[:, cols], in_=w1_bf[u][:].rearrange("p e m j -> p (e m j)"))
+        if PEWARM:
+            wbank = opsum.tile([P, V], F32, name="acc")
+            for r in range(PEWARM):
+                nc.tensor.matmul_mx(out=wbank[:, 0 : 2 * P], lhsT=w1c[:, 0:P].bitcast(FP8X4), lhsT_scale=w1s[:, 0:P],
+                                    rhs=w1c[:, 0 : 2 * P].bitcast(FP8X4), rhs_scale=w1s[:, 0 : 2 * P], start=True, stop=True)
+
+        piece = 2 * CH
+        xw_picked = {}
+        for i in GORDER:
+            xw_picked[i] = keep.tile([P, piece], U32, name="xw_picked%d" % i, align_bytes=64)
+            nc.vector.tensor_copy(xw_picked[i][:], xw[:].indirect(lists[:, piece // 16 * i : piece // 16 * (i + 1)]))
 
         def first(dst, t, col):
-            nc.tensor.matmul_mx(out=dst, lhsT=w1c[t][:].bitcast(FP8X4), lhsT_scale=w1s[t][:],
-                                rhs=xw_picked[:, col : col + CH].bitcast(FP8X4), rhs_scale=xs_placed[:, col : col + CH], start=True, stop=True)
+            part = xw_picked[col // piece][:, col % piece : col % piece + CH]
+            nc.tensor.matmul_mx(out=dst, lhsT=w1c[:, P * t : P * (t + 1)].bitcast(FP8X4), lhsT_scale=w1s[:, P * t : P * (t + 1)],
+                                rhs=part.bitcast(FP8X4), rhs_scale=xs_placed[:, col : col + CH], start=True, stop=True)
 
         zmax = {}
-        zbf = {}
+        held = {}
+        group_of = {c: g for g, grp in enumerate(GROUPS) for c in grp}
+        zbf = [keep.tile([P, len(grp) * CH * PACK], BF16, name="zb%d" % g, align_bytes=64) for g, grp in enumerate(GROUPS)]
+        zm = [keep.tile([P, CH * PACK], F32, name="zm%d" % c, align_bytes=64) for c in range(NCH)]
 
-        def products(c):
-            zm = work.tile([P, CH * PACK], F32, name="zm", align_bytes=64)
-            if c in REDUCE_CHUNKS:
-                for u in range(2):
-                    bank = ypsum.tile([P, 2, 2, CH], F32, name="bank")
-                    for e in range(2):
-                        for r in range(2):
-                            first(bank[:, r, e, :], 2 * u + e, V * r + CH * c)
-                    nc.vector.tensor_reduce(zm[:, 2 * CH * u : 2 * CH * (u + 1)].rearrange("p (v e) -> p v e", e=2),
-                                            bank[:].rearrange("p r e v -> p v e r"), AX, MAX)
-                zmax[c] = zm[:].rearrange("p (u v e) -> p v u e", u=2, e=2)
-            else:
-                bank_a = ypsum.tile([P, 2, 2, CH], F32, name="bank")
-                for t in range(PACK):
-                    first(bank_a[:, t // 2, t % 2, :], t, CH * c)
-                ya = work.tile([P, CH, PACK], F32, name="ya", align_bytes=64)
-                nc.scalar.copy(ya[:], bank_a[:].rearrange("p u e v -> p v (u e)"))
-                bank_b = ypsum.tile([P, 2, 2, CH], F32, name="bank")
-                for t in range(PACK):
-                    first(bank_b[:, t // 2, t % 2, :], t, V + CH * c)
-                nc.vector.tensor_tensor(zm[:].rearrange("p (v t) -> p v t", t=PACK), bank_b[:].rearrange("p u e v -> p v (u e)"), ya[:], MAX)
-                zmax[c] = zm[:].rearrange("p (v u e) -> p v u e", u=2, e=2)
+        def both(c, u):
+            bank = ypsum.tile([P, 2, 2, CH], F32, name="bank")
+            for e in range(2):
+                for r in range(2):
+                    first(bank[:, r, e, :], 2 * u + e, V * r + CH * c)
+            nc.vector.tensor_reduce(zm[c][:, 2 * CH * u : 2 * CH * (u + 1)].rearrange("p (v e) -> p v e", e=2),
+                                    bank[:].rearrange("p r e v -> p v e r"), AX, MAX)
+            zmax[c] = zm[c][:].rearrange("p (u v e) -> p v u e", u=2, e=2)
+
+        def read_a(c):
+            bank_a = ypsum.tile([P, 2, 2, CH], F32, name="bank")
+            for t in range(PACK):
+                first(bank_a[:, t // 2, t % 2, :], t, CH * c)
+            ya = work.tile([P, CH, PACK], F32, name="ya", align_bytes=64)
+            nc.scalar.copy(ya[:], bank_a[:].rearrange("p u e v -> p v (u e)"))
+            held[c] = ya
+
+        def read_b(c):
+            bank_b = ypsum.tile([P, 2, 2, CH], F32, name="bank")
+            for t in range(PACK):
+                first(bank_b[:, t // 2, t % 2, :], t, V + CH * c)
+            nc.vector.tensor_tensor(zm[c][:].rearrange("p (v t) -> p v t", t=PACK), bank_b[:].rearrange("p u e v -> p v (u e)"), held[c][:], MAX)
+            zmax[c] = zm[c][:].rearrange("p (v u e) -> p v u e", u=2, e=2)
 
         def activate(c):
-            zb = work.tile([P, CH * PACK], BF16, name="zb", align_bytes=64)
-            nc.scalar.activation(zb[:].rearrange("p (v u e) -> p v u e", u=2, e=2), zmax[c], GELU)
-            zbf[c] = zb
+            g = group_of[c]
+            i = c - GROUPS[g][0]
+            nc.scalar.activation(zbf[g][:, i * CH * PACK : (i + 1) * CH * PACK].rearrange("p (v u e) -> p v u e", u=2, e=2), zmax[c], GELU, bias=warm[:])
 
-        def second(c):
-            zc = work.tile([P, CH], U32, name="zc", align_bytes=64)
-            zs = work.tile([P, CH], U8, name="zs", align_bytes=64)
-            nc.vector.quantize_mx(out=zc[:].bitcast(FP8X4), scales=zs[:], in_=zbf[c][:])
-            acc = opsum.tile([P, CH], F32, name="acc")
-            nc.tensor.matmul_mx(out=acc[:], lhsT=w2w[:].bitcast(FP8X4), lhsT_scale=w2s[:], rhs=zc[:].bitcast(FP8X4), rhs_scale=zs[:], start=True, stop=True)
-            res = work.tile([P, CH], F32, name="res", align_bytes=64)
-            if c in OUT_ON_SCALAR:
-                nc.scalar.copy(res[:], acc[:])
+        def second(g):
+            w = CH * len(GROUPS[g])
+            c0 = CH * GROUPS[g][0]
+            zc = keep.tile([P, w], U32, name="zc%d" % g, align_bytes=64)
+            zs = keep.tile([P, w], U8, name="zs%d" % g, align_bytes=64)
+            nc.vector.quantize_mx(out=zc[:].bitcast(FP8X4), scales=zs[:], in_=zbf[g][:])
+            acc = opsum.tile([P, V], F32, name="acc")
+            nc.tensor.matmul_mx(out=acc[:, 0:w], lhsT=w2w[:].bitcast(FP8X4), lhsT_scale=w2s[:], rhs=zc[:].bitcast(FP8X4), rhs_scale=zs[:], start=True, stop=True)
+            held["acc", g] = acc
+
+        def leave(g):
+            w = CH * len(GROUPS[g])
+            c0 = CH * GROUPS[g][0]
+            acc = held["acc", g]
+            res = keep.tile([P, w], F32, name="res%d" % g, align_bytes=64)
+            if g in OUT_ON_SCALAR:
+                nc.scalar.copy(res[:], acc[:, 0:w])
             else:
-                nc.vector.tensor_copy(res[:], acc[:])
-            nc.sync.dma_start(out[:, CH * c : CH * (c + 1)], res[:])
+                nc.vector.tensor_copy(res[:], acc[:, 0:w])
+            nc.sync.dma_start(out[:, c0 : c0 + w], res[:])
 
-        for step in range(NCH + 2):
-            if step < NCH:
-                products(step)
-            if 0 <= step - 1 < NCH:
-                activate(step - 1)
-            if 0 <= step - 2 < NCH:
-                second(step - 2)
+        for word in ORDER.split():
+            kind, c = word[0], int(word[1])
+            if kind == "a":
+                read_a(c)
+            elif kind == "b":
+                read_b(c)
+            elif kind == "u":
+                both(c, 0)
+            elif kind == "v":
+                both(c, 1)
+            elif kind == "g":
+                activate(c)
+            elif kind == "q":
+                second(c)
+            else:
+                leave(c)

@@ -20,14 +20,12 @@ P = 128
 PACK = 4
 CH = 128
 NCH = V // CH
-REDUCE_CHUNKS = ()
-PEWARM = 4
+PEWARM = 2
 GROUPS = ((0, 1), (2,), (3,))
-ORDER = "a0 a1 a2 b0 a3 b1 g0 b2 g1 b3 g2 q0 g3 q1 o0 q2 o1 o2"
-REPL = True
+ORDER = "a0 a1 a2 b0 p3 b1 g0 b2 g1 v3 g2 q0 g3 q1 q2 o0 o1 o2"
 GORDER = (0, 1, 2, 3)
 WARM = True
-OUT_ON_SCALAR = (1, 2)
+OUT_ON_SCALAR = (0, 1)
 
 
 def tile_picked_phpool_gelu_p_kernel(tc, x_words, x_scales, w1, w2_words, w2_scales, offs, out):
@@ -45,14 +43,12 @@ def tile_picked_phpool_gelu_p_kernel(tc, x_words, x_scales, w1, w2_words, w2_sca
         w1_rows = w1.rearrange("(p j) c -> p j c", j=PACK)
         w1_raw = keep.tile([P, PACK, H], F32, name="w1_raw", align_bytes=64)
         xs = shared.tile([P, T], U8, name="xs", align_bytes=64, offset=0)
-        if REPL:
-            nc.sync.dma_start(xs[:].bitcast(I32), x_scales[0].bitcast(I32).unsqueeze(1).to_broadcast([16, 8, T // 4]))
-            nc.sync.dma_start(w1_raw[:], w1_rows)
-        else:
-            nc.sync.dma_start(w1_raw[:, 0:1], w1_rows[:, 0:1])
-            nc.vector.memset(xs[:].bitcast(I32), 0)
-            nc.sync.dma_start(xs[:].bitcast(I32)[0:P:8, :], x_scales[0].bitcast(I32))
-            nc.sync.dma_start(w1_raw[:, 1:PACK], w1_rows[:, 1:PACK])
+        nc.vector.memset(xs[:].bitcast(I32)[:, 0:320], 0)
+        nc.gpsimd.memset(xs[:].bitcast(I32)[:, 320 : T // 4], 0)
+        nc.sync.dma_start(w1_raw[:, 0:1], w1_rows[:, 0:1])
+        nc.sync.dma_start(xs[:].bitcast(I32)[0:P:8, :], x_scales[0].bitcast(I32))
+        nc.sync.dma_start(w1_raw[:, 1:2], w1_rows[:, 1:2])
+        nc.sync.dma_start(w1_raw[:, 2:PACK], w1_rows[:, 2:PACK])
         xw = keep.tile([P, T], U32, name="xw", align_bytes=64)
         nc.sync.dma_start(xw[:].bitcast(I32), x_words[0].rearrange("p n t -> p (n t)").bitcast(I32))
 
@@ -72,17 +68,16 @@ def tile_picked_phpool_gelu_p_kernel(tc, x_words, x_scales, w1, w2_words, w2_sca
         for j in range(4):
             nc.sync.dma_start(xs_placed[:].bitcast(I32)[j:P:32, :], xs_picked[:].bitcast(I32)[8 * j : P : 32, :])
         w2s = shared.tile([P, N], U8, name="w2s", align_bytes=64, offset=0)
-        nc.vector.memset(w2s[:].bitcast(I32), 0)
-        for q in range(4):
-            nc.sync.dma_start(w2s[:].bitcast(I32)[32 * q : 32 * q + 4, :], w2_scales[0].bitcast(I32)[4 * q : 4 * q + 4, :])
+        for j in range(4):
+            nc.sync.dma_start(w2s[:].bitcast(I32)[j:P:4, :], w2_scales[0].bitcast(I32)[j:16:4, :].unsqueeze(1).to_broadcast([4, 8, N // 4]))
 
         w1_bf = [keep.tile([P, 2, P, PACK], BF16, name="w1_bf%d" % u, align_bytes=64) for u in range(2)]
         w1c = keep.tile([P, H], U32, name="w1c", align_bytes=64)
         w1s = keep.tile([P, H], U8, name="w1s", align_bytes=64)
-        for u in (1, 0):
-            src = w1_raw[:].rearrange("p j (m u e) -> p u m j e", u=2, e=2)[:, u]
-            dst = w1_bf[u][:].rearrange("p e m j -> p m j e")
-            if u == 1:
+        for u, m0, m1, on_scalar in ((0, 0, P, True), (1, 0, 112, False), (1, 112, P, True)):
+            src = w1_raw[:].rearrange("p j (m u e) -> p u m j e", u=2, e=2)[:, u, m0:m1]
+            dst = w1_bf[u][:, :, m0:m1, :].rearrange("p e m j -> p m j e")
+            if on_scalar:
                 nc.scalar.copy(dst, src)
             else:
                 nc.vector.tensor_copy(dst, src)
@@ -91,9 +86,9 @@ def tile_picked_phpool_gelu_p_kernel(tc, x_words, x_scales, w1, w2_words, w2_sca
             nc.vector.quantize_mx(out=w1c[:, cols].bitcast(FP8X4), scales=w1s[:, cols], in_=w1_bf[u][:].rearrange("p e m j -> p (e m j)"))
         if PEWARM:
             wbank = opsum.tile([P, V], F32, name="acc")
-            for r in range(PEWARM):
-                nc.tensor.matmul_mx(out=wbank[:, 0 : 2 * P], lhsT=w1c[:, 0:P].bitcast(FP8X4), lhsT_scale=w1s[:, 0:P],
-                                    rhs=w1c[:, 0 : 2 * P].bitcast(FP8X4), rhs_scale=w1s[:, 0 : 2 * P], start=True, stop=True)
+            for c1 in (2 * P, 2 * P, H):
+                nc.tensor.matmul_mx(out=wbank[:, 0:c1], lhsT=w1c[:, 0:P].bitcast(FP8X4), lhsT_scale=w1s[:, 0:P],
+                                    rhs=w1c[:, 0:c1].bitcast(FP8X4), rhs_scale=w1s[:, 0:c1], start=True, stop=True)
 
         piece = 2 * CH
         xw_picked = {}
@@ -119,6 +114,16 @@ def tile_picked_phpool_gelu_p_kernel(tc, x_words, x_scales, w1, w2_words, w2_sca
                     first(bank[:, r, e, :], 2 * u + e, V * r + CH * c)
             nc.vector.tensor_reduce(zm[c][:, 2 * CH * u : 2 * CH * (u + 1)].rearrange("p (v e) -> p v e", e=2),
                                     bank[:].rearrange("p r e v -> p v e r"), AX, MAX)
+            zmax[c] = zm[c][:].rearrange("p (u v e) -> p v u e", u=2, e=2)
+
+        def pair(c, u):
+            bank = ypsum.tile([P, 2, 2, CH], F32, name="bank")
+            for e in range(2):
+                for r in range(2):
+                    first(bank[:, r, e, :], 2 * u + e, V * r + CH * c)
+            ya = work.tile([P, CH, 2], F32, name="yh", align_bytes=64)
+            nc.scalar.copy(ya[:], bank[:, 0].rearrange("p e v -> p v e"))
+            nc.vector.tensor_tensor(zm[c][:, 2 * CH * u : 2 * CH * (u + 1)].rearrange("p (v e) -> p v e", e=2), bank[:, 1].rearrange("p e v -> p v e"), ya[:], MAX)
             zmax[c] = zm[c][:].rearrange("p (u v e) -> p v u e", u=2, e=2)
 
         def read_a(c):
@@ -172,6 +177,10 @@ def tile_picked_phpool_gelu_p_kernel(tc, x_words, x_scales, w1, w2_words, w2_sca
                 both(c, 0)
             elif kind == "v":
                 both(c, 1)
+            elif kind == "p":
+                pair(c, 0)
+            elif kind == "r":
+                pair(c, 1)
             elif kind == "g":
                 activate(c)
             elif kind == "q":

@@ -21,8 +21,10 @@ PACK = 4
 CH = 128
 NCH = V // CH
 PEWARM = 2
-GROUPS = ((0, 1), (2,), (3,))
-ORDER = "a0 a1 a2 b0 p3 b1 g0 b2 g1 v3 g2 q0 g3 q1 q2 o0 o1 o2"
+BYTE_PARTS = ((0, 768), (768, S))
+GROUPS = ((0, 256), (256, 384), (384, 448), (448, 512))
+STORES = ((0, 256), (256, 512))
+ORDER = "a0 a1 a2 b0 b1 g0 b2 g1 h30 h31 g2 k30 k31 q0 q1 q2 q3 o0 o1 o2 o3"
 GORDER = (0, 1, 2, 3)
 WARM = True
 OUT_ON_SCALAR = (0, 1)
@@ -34,8 +36,8 @@ def tile_picked_phpool_gelu_p_kernel(tc, x_words, x_scales, w1, w2_words, w2_sca
         keep = ctx.enter_context(tc.tile_pool(name="keep", bufs=1))
         shared = ctx.enter_context(tc.tile_pool(name="shared", bufs=1))
         work = ctx.enter_context(tc.tile_pool(name="work", bufs=4))
-        ypsum = ctx.enter_context(tc.psum_pool(name="ypsum", bufs=5))
-        opsum = ctx.enter_context(tc.psum_pool(name="opsum", bufs=3))
+        ypsum = ctx.enter_context(tc.psum_pool(name="ypsum", bufs=4))
+        opsum = ctx.enter_context(tc.psum_pool(name="opsum", bufs=4))
 
         lists = keep.tile([P, S // 16], U16, name="lists")
         nc.sync.dma_start(lists[:], offs)
@@ -58,15 +60,17 @@ def tile_picked_phpool_gelu_p_kernel(tc, x_words, x_scales, w1, w2_words, w2_sca
             warm = keep.tile([P, 1], F32, name="warm")
             nc.scalar.activation(warm[:], zero[:], GELU)
 
-        xs_placed = keep.tile([P, S], U8, name="xs_placed", align_bytes=64)
-        nc.vector.memset(xs_placed[:].bitcast(I32), 0)
-        w2w = keep.tile([P, N], U32, name="w2w", align_bytes=64)
+        placed = []
+        for i, (c0, c1) in enumerate(BYTE_PARTS):
+            placed.append(keep.tile([P, c1 - c0], U8, name="xs_placed%d" % i, align_bytes=64))
+            nc.vector.memset(placed[i][:].bitcast(I32), 0)
+        for i, (c0, c1) in enumerate(BYTE_PARTS):
+            picked = keep.tile([P, c1 - c0], U8, name="xs_picked%d" % i, align_bytes=64)
+            nc.vector.tensor_copy(picked[:], xs[:].indirect(lists[:, c0 // 16 : c1 // 16]))
+            for j in range(4):
+                nc.sync.dma_start(placed[i][:].bitcast(I32)[j:P:32, :], picked[:].bitcast(I32)[8 * j : P : 32, :])
+        w2w = shared.tile([P, N], U32, name="w2w", align_bytes=64, offset=128)
         nc.sync.dma_start(w2w[:].bitcast(I32), w2_words[0].rearrange("p n t -> p (n t)").bitcast(I32))
-
-        xs_picked = keep.tile([P, S], U8, name="xs_picked", align_bytes=64)
-        nc.vector.tensor_copy(xs_picked[:], xs[:].indirect(lists[:]))
-        for j in range(4):
-            nc.sync.dma_start(xs_placed[:].bitcast(I32)[j:P:32, :], xs_picked[:].bitcast(I32)[8 * j : P : 32, :])
         w2s = shared.tile([P, N], U8, name="w2s", align_bytes=64, offset=0)
         for j in range(4):
             nc.sync.dma_start(w2s[:].bitcast(I32)[j:P:4, :], w2_scales[0].bitcast(I32)[j:16:4, :].unsqueeze(1).to_broadcast([4, 8, N // 4]))
@@ -74,7 +78,7 @@ def tile_picked_phpool_gelu_p_kernel(tc, x_words, x_scales, w1, w2_words, w2_sca
         w1_bf = [keep.tile([P, 2, P, PACK], BF16, name="w1_bf%d" % u, align_bytes=64) for u in range(2)]
         w1c = keep.tile([P, H], U32, name="w1c", align_bytes=64)
         w1s = keep.tile([P, H], U8, name="w1s", align_bytes=64)
-        for u, m0, m1, on_scalar in ((0, 0, P, True), (1, 0, 112, False), (1, 112, P, True)):
+        for u, m0, m1, on_scalar in ((0, 0, P, True), (1, 0, 96, False), (1, 96, P, True)):
             src = w1_raw[:].rearrange("p j (m u e) -> p u m j e", u=2, e=2)[:, u, m0:m1]
             dst = w1_bf[u][:, :, m0:m1, :].rearrange("p e m j -> p m j e")
             if on_scalar:
@@ -96,16 +100,33 @@ def tile_picked_phpool_gelu_p_kernel(tc, x_words, x_scales, w1, w2_words, w2_sca
             xw_picked[i] = keep.tile([P, piece], U32, name="xw_picked%d" % i, align_bytes=64)
             nc.vector.tensor_copy(xw_picked[i][:], xw[:].indirect(lists[:, piece // 16 * i : piece // 16 * (i + 1)]))
 
-        def first(dst, t, col):
-            part = xw_picked[col // piece][:, col % piece : col % piece + CH]
+        def scale_of(col, n):
+            i = 0 if col < BYTE_PARTS[0][1] else 1
+            return placed[i][:, col - BYTE_PARTS[i][0] : col - BYTE_PARTS[i][0] + n]
+
+        def first(dst, t, col, n=CH):
+            part = xw_picked[col // piece][:, col % piece : col % piece + n]
             nc.tensor.matmul_mx(out=dst, lhsT=w1c[:, P * t : P * (t + 1)].bitcast(FP8X4), lhsT_scale=w1s[:, P * t : P * (t + 1)],
-                                rhs=part.bitcast(FP8X4), rhs_scale=xs_placed[:, col : col + CH], start=True, stop=True)
+                                rhs=part.bitcast(FP8X4), rhs_scale=scale_of(col, n), start=True, stop=True)
 
         zmax = {}
         held = {}
-        group_of = {c: g for g, grp in enumerate(GROUPS) for c in grp}
-        zbf = [keep.tile([P, len(grp) * CH * PACK], BF16, name="zb%d" % g, align_bytes=64) for g, grp in enumerate(GROUPS)]
+        zbf = keep.tile([P, V * PACK], BF16, name="zbf", align_bytes=64)
         zm = [keep.tile([P, CH * PACK], F32, name="zm%d" % c, align_bytes=64) for c in range(NCH)]
+        res = [keep.tile([P, c1 - c0], F32, name="res%d" % i, align_bytes=64) for i, (c0, c1) in enumerate(STORES)]
+        HALF = CH // 2
+
+        def half(c, h):
+            bank = ypsum.tile([P, 2, PACK, HALF], F32, name="bank")
+            for t in range(PACK):
+                for r in range(2):
+                    first(bank[:, r, t, :], t, V * r + CH * c + HALF * h, HALF)
+            nc.vector.tensor_reduce(zm[c][:, PACK * HALF * h : PACK * HALF * (h + 1)].rearrange("p (v t) -> p v t", t=PACK),
+                                    bank[:].rearrange("p r t v -> p v t r"), AX, MAX)
+
+        def activate_half(c, h):
+            v0 = CH * c + HALF * h
+            nc.scalar.activation(zbf[:, PACK * v0 : PACK * (v0 + HALF)], zm[c][:, PACK * HALF * h : PACK * HALF * (h + 1)], GELU, bias=warm[:])
 
         def both(c, u):
             bank = ypsum.tile([P, 2, 2, CH], F32, name="bank")
@@ -142,30 +163,28 @@ def tile_picked_phpool_gelu_p_kernel(tc, x_words, x_scales, w1, w2_words, w2_sca
             zmax[c] = zm[c][:].rearrange("p (v u e) -> p v u e", u=2, e=2)
 
         def activate(c):
-            g = group_of[c]
-            i = c - GROUPS[g][0]
-            nc.scalar.activation(zbf[g][:, i * CH * PACK : (i + 1) * CH * PACK].rearrange("p (v u e) -> p v u e", u=2, e=2), zmax[c], GELU, bias=warm[:])
+            nc.scalar.activation(zbf[:, c * CH * PACK : (c + 1) * CH * PACK].rearrange("p (v u e) -> p v u e", u=2, e=2), zmax[c], GELU, bias=warm[:])
 
         def second(g):
-            w = CH * len(GROUPS[g])
-            c0 = CH * GROUPS[g][0]
+            c0, c1 = GROUPS[g]
+            w = c1 - c0
             zc = keep.tile([P, w], U32, name="zc%d" % g, align_bytes=64)
             zs = keep.tile([P, w], U8, name="zs%d" % g, align_bytes=64)
-            nc.vector.quantize_mx(out=zc[:].bitcast(FP8X4), scales=zs[:], in_=zbf[g][:])
+            nc.vector.quantize_mx(out=zc[:].bitcast(FP8X4), scales=zs[:], in_=zbf[:, PACK * c0 : PACK * c1])
             acc = opsum.tile([P, V], F32, name="acc")
             nc.tensor.matmul_mx(out=acc[:, 0:w], lhsT=w2w[:].bitcast(FP8X4), lhsT_scale=w2s[:], rhs=zc[:].bitcast(FP8X4), rhs_scale=zs[:], start=True, stop=True)
             held["acc", g] = acc
 
         def leave(g):
-            w = CH * len(GROUPS[g])
-            c0 = CH * GROUPS[g][0]
-            acc = held["acc", g]
-            res = keep.tile([P, w], F32, name="res%d" % g, align_bytes=64)
+            c0, c1 = GROUPS[g]
+            i = [k for k, (s0, s1) in enumerate(STORES) if s0 <= c0 < s1][0]
+            s0, s1 = STORES[i]
             if g in OUT_ON_SCALAR:
-                nc.scalar.copy(res[:], acc[:, 0:w])
+                nc.scalar.copy(res[i][:, c0 - s0 : c1 - s0], held["acc", g][:, 0 : c1 - c0])
             else:
-                nc.vector.tensor_copy(res[:], acc[:, 0:w])
-            nc.sync.dma_start(out[:, c0 : c0 + w], res[:])
+                nc.vector.tensor_copy(res[i][:, c0 - s0 : c1 - s0], held["acc", g][:, 0 : c1 - c0])
+            if c1 == s1:
+                nc.sync.dma_start(out[:, s0:s1], res[i][:])
 
         for word in ORDER.split():
             kind, c = word[0], int(word[1])
@@ -181,6 +200,10 @@ def tile_picked_phpool_gelu_p_kernel(tc, x_words, x_scales, w1, w2_words, w2_sca
                 pair(c, 0)
             elif kind == "r":
                 pair(c, 1)
+            elif kind == "h":
+                half(c, int(word[2]))
+            elif kind == "k":
+                activate_half(c, int(word[2]))
             elif kind == "g":
                 activate(c)
             elif kind == "q":

@@ -24,7 +24,7 @@ PEWARM = 2
 BYTE_PARTS = ((0, 768), (768, S))
 GROUPS = ((0, 256), (256, 384), (384, 448), (448, 512))
 STORES = ((0, 256), (256, 512))
-ORDER = "a0 a1 a2 b0 b1 g0 b2 g1 h30 h31 g2 k30 k31 q0 q1 q2 q3 o0 o1 o2 o3"
+ORDER = "a0 a1 a2 b0 b1 g0 b2 g1 h30 h31 g2 k30 k31 q0 q1 q2 q3 o0 o1 o2"
 GORDER = (0, 1, 2, 3)
 WARM = True
 OUT_ON_SCALAR = (0, 1)
@@ -36,21 +36,21 @@ def tile_picked_phpool_gelu_p_kernel(tc, x_words, x_scales, w1, w2_words, w2_sca
         keep = ctx.enter_context(tc.tile_pool(name="keep", bufs=1))
         shared = ctx.enter_context(tc.tile_pool(name="shared", bufs=1))
         work = ctx.enter_context(tc.tile_pool(name="work", bufs=4))
-        ypsum = ctx.enter_context(tc.psum_pool(name="ypsum", bufs=4))
-        opsum = ctx.enter_context(tc.psum_pool(name="opsum", bufs=4))
+        ypsum = ctx.enter_context(tc.psum_pool(name="ypsum", bufs=5))
+        opsum = ctx.enter_context(tc.psum_pool(name="opsum", bufs=3))
 
         lists = keep.tile([P, S // 16], U16, name="lists")
         nc.sync.dma_start(lists[:], offs)
 
         w1_rows = w1.rearrange("(p j) c -> p j c", j=PACK)
-        w1_raw = keep.tile([P, PACK, H], F32, name="w1_raw", align_bytes=64)
+        w1_raw = [keep.tile([P, 2, H], F32, name="w1_raw%d" % h, align_bytes=64) for h in range(2)]
         xs = shared.tile([P, T], U8, name="xs", align_bytes=64, offset=0)
         nc.vector.memset(xs[:].bitcast(I32)[:, 0:320], 0)
         nc.gpsimd.memset(xs[:].bitcast(I32)[:, 320 : T // 4], 0)
-        nc.sync.dma_start(w1_raw[:, 0:1], w1_rows[:, 0:1])
+        nc.sync.dma_start(w1_raw[0][:, 0:1], w1_rows[:, 0:1])
         nc.sync.dma_start(xs[:].bitcast(I32)[0:P:8, :], x_scales[0].bitcast(I32))
-        nc.sync.dma_start(w1_raw[:, 1:2], w1_rows[:, 1:2])
-        nc.sync.dma_start(w1_raw[:, 2:PACK], w1_rows[:, 2:PACK])
+        nc.sync.dma_start(w1_raw[0][:, 1:2], w1_rows[:, 1:2])
+        nc.sync.dma_start(w1_raw[1][:], w1_rows[:, 2:PACK])
         xw = keep.tile([P, T], U32, name="xw", align_bytes=64)
         nc.sync.dma_start(xw[:].bitcast(I32), x_words[0].rearrange("p n t -> p (n t)").bitcast(I32))
 
@@ -78,9 +78,9 @@ def tile_picked_phpool_gelu_p_kernel(tc, x_words, x_scales, w1, w2_words, w2_sca
         w1_bf = [keep.tile([P, 2, P, PACK], BF16, name="w1_bf%d" % u, align_bytes=64) for u in range(2)]
         w1c = keep.tile([P, H], U32, name="w1c", align_bytes=64)
         w1s = keep.tile([P, H], U8, name="w1s", align_bytes=64)
-        for u, m0, m1, on_scalar in ((0, 0, P, True), (1, 0, 96, False), (1, 96, P, True)):
-            src = w1_raw[:].rearrange("p j (m u e) -> p u m j e", u=2, e=2)[:, u, m0:m1]
-            dst = w1_bf[u][:, :, m0:m1, :].rearrange("p e m j -> p m j e")
+        for h, u, m0, m1, on_scalar in ((0, 0, 0, P, True), (1, 0, 0, P, True), (0, 1, 0, P, False), (1, 1, 0, P, True)):
+            src = w1_raw[h][:].rearrange("p j (m u e) -> p u m j e", u=2, e=2)[:, u, m0:m1]
+            dst = w1_bf[u][:, :, m0:m1, 2 * h : 2 * h + 2].rearrange("p e m j -> p m j e")
             if on_scalar:
                 nc.scalar.copy(dst, src)
             else:
@@ -90,8 +90,8 @@ def tile_picked_phpool_gelu_p_kernel(tc, x_words, x_scales, w1, w2_words, w2_sca
             nc.vector.quantize_mx(out=w1c[:, cols].bitcast(FP8X4), scales=w1s[:, cols], in_=w1_bf[u][:].rearrange("p e m j -> p (e m j)"))
         if PEWARM:
             wbank = opsum.tile([P, V], F32, name="acc")
-            for c1 in (2 * P, 2 * P, H):
-                nc.tensor.matmul_mx(out=wbank[:, 0:c1], lhsT=w1c[:, 0:P].bitcast(FP8X4), lhsT_scale=w1s[:, 0:P],
+            for m, c1 in ((P, 2 * P), (P, 2 * P), (P, 2 * P), (32, H)):
+                nc.tensor.matmul_mx(out=wbank[0:m, 0:c1], lhsT=w1c[:, 0:m].bitcast(FP8X4), lhsT_scale=w1s[:, 0:m],
                                     rhs=w1c[:, 0:c1].bitcast(FP8X4), rhs_scale=w1s[:, 0:c1], start=True, stop=True)
 
         piece = 2 * CH
@@ -171,12 +171,14 @@ def tile_picked_phpool_gelu_p_kernel(tc, x_words, x_scales, w1, w2_words, w2_sca
             zc = keep.tile([P, w], U32, name="zc%d" % g, align_bytes=64)
             zs = keep.tile([P, w], U8, name="zs%d" % g, align_bytes=64)
             nc.vector.quantize_mx(out=zc[:].bitcast(FP8X4), scales=zs[:], in_=zbf[:, PACK * c0 : PACK * c1])
-            acc = opsum.tile([P, V], F32, name="acc")
-            nc.tensor.matmul_mx(out=acc[:, 0:w], lhsT=w2w[:].bitcast(FP8X4), lhsT_scale=w2s[:], rhs=zc[:].bitcast(FP8X4), rhs_scale=zs[:], start=True, stop=True)
-            held["acc", g] = acc
+            if g < 3:
+                held["acc", g] = opsum.tile([P, V], F32, name="acc")
+            acc = held["acc", min(g, 2)]
+            at = HALF if g == 3 else 0
+            nc.tensor.matmul_mx(out=acc[:, at : at + w], lhsT=w2w[:].bitcast(FP8X4), lhsT_scale=w2s[:], rhs=zc[:].bitcast(FP8X4), rhs_scale=zs[:], start=True, stop=True)
 
         def leave(g):
-            c0, c1 = GROUPS[g]
+            c0, c1 = GROUPS[g][0], GROUPS[g + (g == 2)][1]
             i = [k for k, (s0, s1) in enumerate(STORES) if s0 <= c0 < s1][0]
             s0, s1 = STORES[i]
             if g in OUT_ON_SCALAR:

@@ -24,8 +24,8 @@ PEWARM = 2
 BYTE_PARTS = ((0, 768), (768, S))
 GROUPS = ((0, 256), (256, 384), (384, 448), (448, 512))
 STORES = ((0, 256), (256, 512))
-ORDER = "a0 a1 a2 b0 b1 g0 b2 g1 h30 h31 g2 k30 k31 q0 q1 q2 q3 o0 o1 o2"
-GORDER = (0, 1, 2, 3)
+ORDER = "a0 a1 b0 b1 a2 g0 b2 g1 h30 h31 g2 k30 k31 q0 q1 q2 q3 o0 o1 o2 o3"
+GORDER = (0, 2, 1, 3)
 WARM = True
 OUT_ON_SCALAR = (0, 1)
 
@@ -35,9 +35,9 @@ def tile_picked_phpool_gelu_p_kernel(tc, x_words, x_scales, w1, w2_words, w2_sca
     with ExitStack() as ctx:
         keep = ctx.enter_context(tc.tile_pool(name="keep", bufs=1))
         shared = ctx.enter_context(tc.tile_pool(name="shared", bufs=1))
+        reuse = ctx.enter_context(tc.tile_pool(name="reuse", bufs=1))
         work = ctx.enter_context(tc.tile_pool(name="work", bufs=4))
-        ypsum = ctx.enter_context(tc.psum_pool(name="ypsum", bufs=5))
-        opsum = ctx.enter_context(tc.psum_pool(name="opsum", bufs=3))
+        ypsum = ctx.enter_context(tc.psum_pool(name="ypsum", bufs=8))
 
         lists = keep.tile([P, S // 16], U16, name="lists")
         nc.sync.dma_start(lists[:], offs)
@@ -45,8 +45,7 @@ def tile_picked_phpool_gelu_p_kernel(tc, x_words, x_scales, w1, w2_words, w2_sca
         w1_rows = w1.rearrange("(p j) c -> p j c", j=PACK)
         w1_raw = [keep.tile([P, 2, H], F32, name="w1_raw%d" % h, align_bytes=64) for h in range(2)]
         xs = shared.tile([P, T], U8, name="xs", align_bytes=64, offset=0)
-        nc.vector.memset(xs[:].bitcast(I32)[:, 0:320], 0)
-        nc.gpsimd.memset(xs[:].bitcast(I32)[:, 320 : T // 4], 0)
+        nc.vector.memset(xs[:].bitcast(I32), 0)
         nc.sync.dma_start(w1_raw[0][:, 0:1], w1_rows[:, 0:1])
         nc.sync.dma_start(xs[:].bitcast(I32)[0:P:8, :], x_scales[0].bitcast(I32))
         nc.sync.dma_start(w1_raw[0][:, 1:2], w1_rows[:, 1:2])
@@ -69,13 +68,8 @@ def tile_picked_phpool_gelu_p_kernel(tc, x_words, x_scales, w1, w2_words, w2_sca
             nc.vector.tensor_copy(picked[:], xs[:].indirect(lists[:, c0 // 16 : c1 // 16]))
             for j in range(4):
                 nc.sync.dma_start(placed[i][:].bitcast(I32)[j:P:32, :], picked[:].bitcast(I32)[8 * j : P : 32, :])
-        w2w = shared.tile([P, N], U32, name="w2w", align_bytes=64, offset=128)
-        nc.sync.dma_start(w2w[:].bitcast(I32), w2_words[0].rearrange("p n t -> p (n t)").bitcast(I32))
-        w2s = shared.tile([P, N], U8, name="w2s", align_bytes=64, offset=0)
-        for j in range(4):
-            nc.sync.dma_start(w2s[:].bitcast(I32)[j:P:4, :], w2_scales[0].bitcast(I32)[j:16:4, :].unsqueeze(1).to_broadcast([4, 8, N // 4]))
 
-        w1_bf = [keep.tile([P, 2, P, PACK], BF16, name="w1_bf%d" % u, align_bytes=64) for u in range(2)]
+        w1_bf = [reuse.tile([P, 2, P, PACK], BF16, name="w1_bf%d" % u, align_bytes=64, offset=2048 * u) for u in range(2)]
         w1c = keep.tile([P, H], U32, name="w1c", align_bytes=64)
         w1s = keep.tile([P, H], U8, name="w1s", align_bytes=64)
         for h, u, m0, m1, on_scalar in ((0, 0, 0, P, True), (1, 0, 0, P, True), (0, 1, 0, P, False), (1, 1, 0, P, True)):
@@ -88,8 +82,13 @@ def tile_picked_phpool_gelu_p_kernel(tc, x_words, x_scales, w1, w2_words, w2_sca
         for u in (0, 1):
             cols = slice(2 * P * u, 2 * P * (u + 1))
             nc.vector.quantize_mx(out=w1c[:, cols].bitcast(FP8X4), scales=w1s[:, cols], in_=w1_bf[u][:].rearrange("p e m j -> p (e m j)"))
+        w2w = reuse.tile([P, N], U32, name="w2w", align_bytes=64, offset=2048 + 128)
+        nc.sync.dma_start(w2w[:].bitcast(I32), w2_words[0].rearrange("p n t -> p (n t)").bitcast(I32))
+        w2s = reuse.tile([P, N], U8, name="w2s", align_bytes=64, offset=2048)
+        for j in range(4):
+            nc.sync.dma_start(w2s[:].bitcast(I32)[j:P:4, :], w2_scales[0].bitcast(I32)[j:16:4, :].unsqueeze(1).to_broadcast([4, 8, N // 4]))
         if PEWARM:
-            wbank = opsum.tile([P, V], F32, name="acc")
+            wbank = ypsum.tile([P, V], F32, name="bank")
             for m, c1 in ((P, 2 * P), (P, 2 * P), (P, 2 * P), (32, H)):
                 nc.tensor.matmul_mx(out=wbank[0:m, 0:c1], lhsT=w1c[:, 0:m].bitcast(FP8X4), lhsT_scale=w1s[:, 0:m],
                                     rhs=w1c[:, 0:c1].bitcast(FP8X4), rhs_scale=w1s[:, 0:c1], start=True, stop=True)
@@ -171,14 +170,12 @@ def tile_picked_phpool_gelu_p_kernel(tc, x_words, x_scales, w1, w2_words, w2_sca
             zc = keep.tile([P, w], U32, name="zc%d" % g, align_bytes=64)
             zs = keep.tile([P, w], U8, name="zs%d" % g, align_bytes=64)
             nc.vector.quantize_mx(out=zc[:].bitcast(FP8X4), scales=zs[:], in_=zbf[:, PACK * c0 : PACK * c1])
-            if g < 3:
-                held["acc", g] = opsum.tile([P, V], F32, name="acc")
-            acc = held["acc", min(g, 2)]
-            at = HALF if g == 3 else 0
-            nc.tensor.matmul_mx(out=acc[:, at : at + w], lhsT=w2w[:].bitcast(FP8X4), lhsT_scale=w2s[:], rhs=zc[:].bitcast(FP8X4), rhs_scale=zs[:], start=True, stop=True)
+            acc = ypsum.tile([P, V], F32, name="bank")
+            nc.tensor.matmul_mx(out=acc[:, 0:w], lhsT=w2w[:].bitcast(FP8X4), lhsT_scale=w2s[:], rhs=zc[:].bitcast(FP8X4), rhs_scale=zs[:], start=True, stop=True)
+            held["acc", g] = acc
 
         def leave(g):
-            c0, c1 = GROUPS[g][0], GROUPS[g + (g == 2)][1]
+            c0, c1 = GROUPS[g]
             i = [k for k, (s0, s1) in enumerate(STORES) if s0 <= c0 < s1][0]
             s0, s1 = STORES[i]
             if g in OUT_ON_SCALAR:

@@ -40,13 +40,12 @@ def tile_picked_phpool_gelu_p_kernel(tc, x_words, x_scales, w1, w2_words, w2_sca
         ypsum = ctx.enter_context(tc.psum_pool(name="ypsum", bufs=8))
 
         lists = keep.tile([P, S // 16], U16, name="lists")
-        nc.sync.dma_start(lists[:], offs)
-
         w1_rows = w1.rearrange("(p j) c -> p j c", j=PACK)
         w1_raw = [keep.tile([P, 2, H], F32, name="w1_raw%d" % h, align_bytes=64) for h in range(2)]
         xs = shared.tile([P, T], U8, name="xs", align_bytes=64, offset=0)
         nc.vector.memset(xs[:].bitcast(I32), 0)
         nc.sync.dma_start(w1_raw[0][:, 0:1], w1_rows[:, 0:1])
+        nc.sync.dma_start(lists[:], offs)
         nc.sync.dma_start(xs[:].bitcast(I32)[0:P:8, :], x_scales[0].bitcast(I32))
         nc.sync.dma_start(w1_raw[0][:, 1:2], w1_rows[:, 1:2])
         nc.sync.dma_start(w1_raw[1][:], w1_rows[:, 2:PACK])
@@ -54,18 +53,23 @@ def tile_picked_phpool_gelu_p_kernel(tc, x_words, x_scales, w1, w2_words, w2_sca
         nc.sync.dma_start(xw[:].bitcast(I32), x_words[0].rearrange("p n t -> p (n t)").bitcast(I32))
 
         if WARM:
-            zero = keep.tile([P, 1], F32, name="zero")
-            nc.vector.memset(zero[:], 0.0)
+            ones = keep.tile([P, PACK * V], BF16, name="ones", align_bytes=64)
+            nc.vector.memset(ones[:].bitcast(I32), 0)
             warm = keep.tile([P, 1], F32, name="warm")
-            nc.scalar.activation(warm[:], zero[:], GELU)
+            nc.scalar.activation(warm[:], ones[:, 0:1], GELU)
+            onec = keep.tile([P, V], U32, name="onec", align_bytes=64)
+            ones_s = keep.tile([P, V], U8, name="ones_s", align_bytes=64)
+            nc.vector.quantize_mx(out=onec[:].bitcast(FP8X4), scales=ones_s[:], in_=ones[:])
 
         placed = []
         for i, (c0, c1) in enumerate(BYTE_PARTS):
             placed.append(keep.tile([P, c1 - c0], U8, name="xs_placed%d" % i, align_bytes=64))
             nc.vector.memset(placed[i][:].bitcast(I32), 0)
+        picks = []
         for i, (c0, c1) in enumerate(BYTE_PARTS):
             picked = keep.tile([P, c1 - c0], U8, name="xs_picked%d" % i, align_bytes=64)
             nc.vector.tensor_copy(picked[:], xs[:].indirect(lists[:, c0 // 16 : c1 // 16]))
+            picks.append(picked)
             for j in range(4):
                 nc.sync.dma_start(placed[i][:].bitcast(I32)[j:P:32, :], picked[:].bitcast(I32)[8 * j : P : 32, :])
 
@@ -89,9 +93,10 @@ def tile_picked_phpool_gelu_p_kernel(tc, x_words, x_scales, w1, w2_words, w2_sca
             nc.sync.dma_start(w2s[:].bitcast(I32)[j:P:4, :], w2_scales[0].bitcast(I32)[j:16:4, :].unsqueeze(1).to_broadcast([4, 8, N // 4]))
         if PEWARM:
             wbank = ypsum.tile([P, V], F32, name="bank")
-            for m, c1 in ((P, 2 * P), (P, 2 * P), (P, 2 * P), (32, H)):
-                nc.tensor.matmul_mx(out=wbank[0:m, 0:c1], lhsT=w1c[:, 0:m].bitcast(FP8X4), lhsT_scale=w1s[:, 0:m],
-                                    rhs=w1c[:, 0:c1].bitcast(FP8X4), rhs_scale=w1s[:, 0:c1], start=True, stop=True)
+            for codes, scales in ((onec[:, 0:32], picks[0][:, 0:32]), (onec[:, 0:32], picks[1][:, 0:32]),
+                                  (w1c[:, 0:32], w1s[:, 0:32]), (w1c[:, 2 * P : 2 * P + 32], w1s[:, 2 * P : 2 * P + 32])):
+                nc.tensor.matmul_mx(out=wbank[0:32, :], lhsT=codes.bitcast(FP8X4), lhsT_scale=scales,
+                                    rhs=onec[:].bitcast(FP8X4), rhs_scale=ones_s[:], start=True, stop=True)
 
         piece = 2 * CH
         xw_picked = {}

@@ -23,11 +23,13 @@ NCH = V // CH
 PEWARM = 2
 BYTE_PARTS = ((0, 768), (768, S))
 GROUPS = ((0, 256), (256, 384), (384, 448), (448, 512))
-STORES = ((0, 256), (256, 512))
+STORES = ((0, 256), (256, 384), (384, 512))
 ORDER = "a0 a1 b0 b1 a2 g0 b2 g1 h30 h31 g2 k30 k31 q0 q1 q2 q3 o0 o1 o2 o3"
 GORDER = (0, 2, 1, 3)
 WARM = True
-OUT_ON_SCALAR = (0, 1)
+LEAD = 704
+SHARE = 32
+OUT_ON_SCALAR = (0,)
 
 
 def tile_picked_phpool_gelu_p_kernel(tc, x_words, x_scales, w1, w2_words, w2_scales, offs, out):
@@ -40,15 +42,14 @@ def tile_picked_phpool_gelu_p_kernel(tc, x_words, x_scales, w1, w2_words, w2_sca
         ypsum = ctx.enter_context(tc.psum_pool(name="ypsum", bufs=8))
 
         lists = keep.tile([P, S // 16], U16, name="lists")
-        w1_rows = w1.rearrange("(p j) c -> p j c", j=PACK)
-        w1_raw = [keep.tile([P, 2, H], F32, name="w1_raw%d" % h, align_bytes=64) for h in range(2)]
+        w1_rows = w1.rearrange("(p j) c -> p (j c)", j=PACK)
+        w1_raw = keep.tile([P, PACK * H], F32, name="w1_raw", align_bytes=64)
         xs = shared.tile([P, T], U8, name="xs", align_bytes=64, offset=0)
         nc.vector.memset(xs[:].bitcast(I32), 0)
-        nc.sync.dma_start(w1_raw[0][:, 0:1], w1_rows[:, 0:1])
+        nc.sync.dma_start(w1_raw[:, 0:LEAD], w1_rows[:, 0:LEAD])
         nc.sync.dma_start(lists[:], offs)
         nc.sync.dma_start(xs[:].bitcast(I32)[0:P:8, :], x_scales[0].bitcast(I32))
-        nc.sync.dma_start(w1_raw[0][:, 1:2], w1_rows[:, 1:2])
-        nc.sync.dma_start(w1_raw[1][:], w1_rows[:, 2:PACK])
+        nc.sync.dma_start(w1_raw[:, LEAD:], w1_rows[:, LEAD:])
         xw = keep.tile([P, T], U32, name="xw", align_bytes=64)
         nc.sync.dma_start(xw[:].bitcast(I32), x_words[0].rearrange("p n t -> p (n t)").bitcast(I32))
 
@@ -68,7 +69,9 @@ def tile_picked_phpool_gelu_p_kernel(tc, x_words, x_scales, w1, w2_words, w2_sca
         picks = []
         for i, (c0, c1) in enumerate(BYTE_PARTS):
             picked = keep.tile([P, c1 - c0], U8, name="xs_picked%d" % i, align_bytes=64)
-            nc.vector.tensor_copy(picked[:], xs[:].indirect(lists[:, c0 // 16 : c1 // 16]))
+            cuts = (c0, 256, c1) if i == 0 else (c0, c1)
+            for g0, g1 in zip(cuts, cuts[1:]):
+                nc.vector.tensor_copy(picked[:, g0 - c0 : g1 - c0], xs[:].indirect(lists[:, g0 // 16 : g1 // 16]))
             picks.append(picked)
             for j in range(4):
                 nc.sync.dma_start(placed[i][:].bitcast(I32)[j:P:32, :], picked[:].bitcast(I32)[8 * j : P : 32, :])
@@ -76,9 +79,9 @@ def tile_picked_phpool_gelu_p_kernel(tc, x_words, x_scales, w1, w2_words, w2_sca
         w1_bf = [reuse.tile([P, 2, P, PACK], BF16, name="w1_bf%d" % u, align_bytes=64, offset=2048 * u) for u in range(2)]
         w1c = keep.tile([P, H], U32, name="w1c", align_bytes=64)
         w1s = keep.tile([P, H], U8, name="w1s", align_bytes=64)
-        for h, u, m0, m1, on_scalar in ((0, 0, 0, P, True), (1, 0, 0, P, True), (0, 1, 0, P, False), (1, 1, 0, P, True)):
-            src = w1_raw[h][:].rearrange("p j (m u e) -> p u m j e", u=2, e=2)[:, u, m0:m1]
-            dst = w1_bf[u][:, :, m0:m1, 2 * h : 2 * h + 2].rearrange("p e m j -> p m j e")
+        for u, m0, m1, on_scalar in ((0, 0, P, True), (1, 0, SHARE, True), (1, SHARE, P, False)):
+            src = w1_raw[:].rearrange("p (j m u e) -> p u m j e", j=PACK, u=2, e=2)[:, u, m0:m1]
+            dst = w1_bf[u][:, :, m0:m1, :].rearrange("p e m j -> p m j e")
             if on_scalar:
                 nc.scalar.copy(dst, src)
             else:
@@ -93,8 +96,8 @@ def tile_picked_phpool_gelu_p_kernel(tc, x_words, x_scales, w1, w2_words, w2_sca
             nc.sync.dma_start(w2s[:].bitcast(I32)[j:P:4, :], w2_scales[0].bitcast(I32)[j:16:4, :].unsqueeze(1).to_broadcast([4, 8, N // 4]))
         if PEWARM:
             wbank = ypsum.tile([P, V], F32, name="bank")
-            for codes, scales in ((onec[:, 0:32], picks[0][:, 0:32]), (onec[:, 0:32], picks[1][:, 0:32]),
-                                  (w1c[:, 0:32], w1s[:, 0:32]), (w1c[:, 2 * P : 2 * P + 32], w1s[:, 2 * P : 2 * P + 32])):
+            for codes, scales in ((onec[:, 0:32], picks[0][:, 0:32]), (onec[:, 0:32], picks[0][:, 0:32]),
+                                  (onec[:, 0:32], picks[1][:, 0:32]), (w1c[:, 0:32], w1s[:, 0:32])):
                 nc.tensor.matmul_mx(out=wbank[0:32, :], lhsT=codes.bitcast(FP8X4), lhsT_scale=scales,
                                     rhs=onec[:].bitcast(FP8X4), rhs_scale=ones_s[:], start=True, stop=True)
 
@@ -127,6 +130,25 @@ def tile_picked_phpool_gelu_p_kernel(tc, x_words, x_scales, w1, w2_words, w2_sca
                     first(bank[:, r, t, :], t, V * r + CH * c + HALF * h, HALF)
             nc.vector.tensor_reduce(zm[c][:, PACK * HALF * h : PACK * HALF * (h + 1)].rearrange("p (v t) -> p v t", t=PACK),
                                     bank[:].rearrange("p r t v -> p v t r"), AX, MAX)
+
+        def copied_half(c, h):
+            bank = ypsum.tile([P, 2, PACK, HALF], F32, name="bank")
+            for r in range(2):
+                for t in range(PACK):
+                    first(bank[:, r, t, :], t, V * r + CH * c + HALF * h, HALF)
+            ya = work.tile([P, HALF, PACK], F32, name="yq", align_bytes=64)
+            nc.scalar.copy(ya[:], bank[:, 0].rearrange("p t v -> p v t"))
+            nc.vector.tensor_tensor(zm[c][:, PACK * HALF * h : PACK * HALF * (h + 1)].rearrange("p (v t) -> p v t", t=PACK),
+                                    bank[:, 1].rearrange("p t v -> p v t"), ya[:], MAX)
+
+        def read_a_split(c):
+            ya = work.tile([P, CH, PACK], F32, name="ya", align_bytes=64)
+            for u in range(2):
+                bank_a = ypsum.tile([P, 2, CH], F32, name="bank")
+                for e in range(2):
+                    first(bank_a[:, e, :], 2 * u + e, CH * c)
+                nc.scalar.copy(ya[:, :, 2 * u : 2 * u + 2], bank_a[:].rearrange("p e v -> p v e"))
+            held[c] = ya
 
         def activate_half(c, h):
             v0 = CH * c + HALF * h
@@ -188,7 +210,8 @@ def tile_picked_phpool_gelu_p_kernel(tc, x_words, x_scales, w1, w2_words, w2_sca
             else:
                 nc.vector.tensor_copy(res[i][:, c0 - s0 : c1 - s0], held["acc", g][:, 0 : c1 - c0])
             if c1 == s1:
-                nc.sync.dma_start(out[:, s0:s1], res[i][:])
+                queue = nc.scalar if i == 0 else nc.sync
+                queue.dma_start(out[:, s0:s1], res[i][:])
 
         for word in ORDER.split():
             kind, c = word[0], int(word[1])
@@ -206,6 +229,10 @@ def tile_picked_phpool_gelu_p_kernel(tc, x_words, x_scales, w1, w2_words, w2_sca
                 pair(c, 1)
             elif kind == "h":
                 half(c, int(word[2]))
+            elif kind == "c":
+                copied_half(c, int(word[2]))
+            elif kind == "s":
+                read_a_split(c)
             elif kind == "k":
                 activate_half(c, int(word[2]))
             elif kind == "g":

@@ -69,7 +69,7 @@ def tile_picked_phpool_gelu_p_kernel(tc, x_words, x_scales, w1, w2_words, w2_sca
         picks = []
         for i, (c0, c1) in enumerate(BYTE_PARTS):
             picked = keep.tile([P, c1 - c0], U8, name="xs_picked%d" % i, align_bytes=64)
-            cuts = (c0, 256, c1) if i == 0 else (c0, c1)
+            cuts = (c0, 512, c1) if i == 0 else (c0, c1)
             for g0, g1 in zip(cuts, cuts[1:]):
                 nc.vector.tensor_copy(picked[:, g0 - c0 : g1 - c0], xs[:].indirect(lists[:, g0 // 16 : g1 // 16]))
             picks.append(picked)
@@ -97,7 +97,7 @@ def tile_picked_phpool_gelu_p_kernel(tc, x_words, x_scales, w1, w2_words, w2_sca
         if PEWARM:
             wbank = ypsum.tile([P, V], F32, name="bank")
             for codes, scales in ((onec[:, 0:32], picks[0][:, 0:32]), (onec[:, 0:32], picks[0][:, 0:32]),
-                                  (onec[:, 0:32], picks[1][:, 0:32]), (w1c[:, 0:32], w1s[:, 0:32])):
+                                  (w1c[:, 0:32], w1s[:, 0:32]), (w1c[:, 2 * P : 2 * P + 32], w1s[:, 2 * P : 2 * P + 32])):
                 nc.tensor.matmul_mx(out=wbank[0:32, :], lhsT=codes.bitcast(FP8X4), lhsT_scale=scales,
                                     rhs=onec[:].bitcast(FP8X4), rhs_scale=ones_s[:], start=True, stop=True)
 
@@ -210,7 +210,7 @@ def tile_picked_phpool_gelu_p_kernel(tc, x_words, x_scales, w1, w2_words, w2_sca
             else:
                 nc.vector.tensor_copy(res[i][:, c0 - s0 : c1 - s0], held["acc", g][:, 0 : c1 - c0])
             if c1 == s1:
-                queue = nc.scalar if i == 0 else nc.sync
+                queue = nc.sync
                 queue.dma_start(out[:, s0:s1], res[i][:])
 
         for word in ORDER.split():

@@ -14,37 +14,37 @@ U8 = mybir.dt.uint8
 FP8X4 = mybir.dt.float8_e4m3fn_x4
 GELU = mybir.ActivationFunctionType.Gelu_apprx_tanh
 MAX = mybir.AluOpType.max
-AX = mybir.AxisListType.X
+AXIS_X = mybir.AxisListType.X
 
 P = 128
 PACK = 4
-CH = 128
-NCH = V // CH
-PEWARM = 2
-BYTE_PARTS = ((0, 768), (768, S))
-GROUPS = ((0, 256), (256, 384), (384, 448), (448, 512))
-STORES = ((0, 256), (256, 384), (384, 512))
-ORDER = "a0 a1 b0 b1 a2 g0 b2 g1 h30 h31 g2 k30 k31 q0 q1 q2 q3 o0 o1 o2 o3"
-GORDER = (0, 2, 1, 3)
-WARM = True
+LANES = 16
+BANK = 512
+
 LEAD = 704
 SHARE = 32
-OUT_ON_SCALAR = (0,)
+BYTE_GATHERS = (((0, 512), (512, 768)), ((768, S),))
+PIECE = 256
+CHUNK = 128
+HALF = 64
+LAST_PIECES = (((0, 64),), ((0, 32), (32, 64)))
+GROUPS = ((0, 128), (128, 256), (256, 384), (384, 448), (448, 512))
+STORE = 128
+GROUPS_ON_SCALAR = 2
+WARM_M = 32
 
 
 def tile_picked_phpool_gelu_p_kernel(tc, x_words, x_scales, w1, w2_words, w2_scales, offs, out):
     nc = tc.nc
     with ExitStack() as ctx:
         keep = ctx.enter_context(tc.tile_pool(name="keep", bufs=1))
-        shared = ctx.enter_context(tc.tile_pool(name="shared", bufs=1))
         reuse = ctx.enter_context(tc.tile_pool(name="reuse", bufs=1))
-        work = ctx.enter_context(tc.tile_pool(name="work", bufs=4))
-        ypsum = ctx.enter_context(tc.psum_pool(name="ypsum", bufs=8))
+        banks = ctx.enter_context(tc.psum_pool(name="banks", bufs=8))
 
-        lists = keep.tile([P, S // 16], U16, name="lists")
+        lists = keep.tile([P, S // LANES], U16, name="lists")
         w1_rows = w1.rearrange("(p j) c -> p (j c)", j=PACK)
         w1_raw = keep.tile([P, PACK * H], F32, name="w1_raw", align_bytes=64)
-        xs = shared.tile([P, T], U8, name="xs", align_bytes=64, offset=0)
+        xs = keep.tile([P, T], U8, name="xs", align_bytes=64)
         nc.vector.memset(xs[:].bitcast(I32), 0)
         nc.sync.dma_start(w1_raw[:, 0:LEAD], w1_rows[:, 0:LEAD])
         nc.sync.dma_start(lists[:], offs)
@@ -53,191 +53,121 @@ def tile_picked_phpool_gelu_p_kernel(tc, x_words, x_scales, w1, w2_words, w2_sca
         xw = keep.tile([P, T], U32, name="xw", align_bytes=64)
         nc.sync.dma_start(xw[:].bitcast(I32), x_words[0].rearrange("p n t -> p (n t)").bitcast(I32))
 
-        if WARM:
-            ones = keep.tile([P, PACK * V], BF16, name="ones", align_bytes=64)
-            nc.vector.memset(ones[:].bitcast(I32), 0)
-            warm = keep.tile([P, 1], F32, name="warm")
-            nc.scalar.activation(warm[:], ones[:, 0:1], GELU)
-            onec = keep.tile([P, V], U32, name="onec", align_bytes=64)
-            ones_s = keep.tile([P, V], U8, name="ones_s", align_bytes=64)
-            nc.vector.quantize_mx(out=onec[:].bitcast(FP8X4), scales=ones_s[:], in_=ones[:])
+        zeros = keep.tile([P, PACK * BANK], BF16, name="zeros", align_bytes=64)
+        nc.vector.memset(zeros[:].bitcast(I32), 0)
+        bias = keep.tile([P, 1], F32, name="bias")
+        nc.scalar.activation(bias[:], zeros[:, 0:1], GELU)
+        warm_words = keep.tile([P, BANK], U32, name="warm_words", align_bytes=64)
+        warm_scales = keep.tile([P, BANK], U8, name="warm_scales", align_bytes=64)
+        nc.vector.quantize_mx(out=warm_words[:].bitcast(FP8X4), scales=warm_scales[:], in_=zeros[:])
 
         placed = []
-        for i, (c0, c1) in enumerate(BYTE_PARTS):
-            placed.append(keep.tile([P, c1 - c0], U8, name="xs_placed%d" % i, align_bytes=64))
-            nc.vector.memset(placed[i][:].bitcast(I32), 0)
-        picks = []
-        for i, (c0, c1) in enumerate(BYTE_PARTS):
-            picked = keep.tile([P, c1 - c0], U8, name="xs_picked%d" % i, align_bytes=64)
-            cuts = (c0, 512, c1) if i == 0 else (c0, c1)
-            for g0, g1 in zip(cuts, cuts[1:]):
-                nc.vector.tensor_copy(picked[:, g0 - c0 : g1 - c0], xs[:].indirect(lists[:, g0 // 16 : g1 // 16]))
-            picks.append(picked)
+        for part, gathers in enumerate(BYTE_GATHERS):
+            placed.append(keep.tile([P, gathers[-1][1] - gathers[0][0]], U8, name="placed%d" % part, align_bytes=64))
+            nc.vector.memset(placed[part][:].bitcast(I32), 0)
+        picked = []
+        for part, gathers in enumerate(BYTE_GATHERS):
+            base = gathers[0][0]
+            picked.append(keep.tile([P, gathers[-1][1] - base], U8, name="picked%d" % part, align_bytes=64))
+            for e0, e1 in gathers:
+                nc.vector.tensor_copy(picked[part][:, e0 - base : e1 - base], xs[:].indirect(lists[:, e0 // LANES : e1 // LANES]))
             for j in range(4):
-                nc.sync.dma_start(placed[i][:].bitcast(I32)[j:P:32, :], picked[:].bitcast(I32)[8 * j : P : 32, :])
+                nc.sync.dma_start(placed[part][:].bitcast(I32)[j:P:32, :], picked[part][:].bitcast(I32)[8 * j : P : 32, :])
 
-        w1_bf = [reuse.tile([P, 2, P, PACK], BF16, name="w1_bf%d" % u, align_bytes=64, offset=2048 * u) for u in range(2)]
-        w1c = keep.tile([P, H], U32, name="w1c", align_bytes=64)
-        w1s = keep.tile([P, H], U8, name="w1s", align_bytes=64)
-        for u, m0, m1, on_scalar in ((0, 0, P, True), (1, 0, SHARE, True), (1, SHARE, P, False)):
-            src = w1_raw[:].rearrange("p (j m u e) -> p u m j e", j=PACK, u=2, e=2)[:, u, m0:m1]
-            dst = w1_bf[u][:, :, m0:m1, :].rearrange("p e m j -> p m j e")
-            if on_scalar:
-                nc.scalar.copy(dst, src)
-            else:
-                nc.vector.tensor_copy(dst, src)
-        for u in (0, 1):
+        pair_bytes = 2 * P * PACK * 2
+        w1_bf = [reuse.tile([P, 2, P, PACK], BF16, name="w1_bf%d" % u, align_bytes=64, offset=pair_bytes * u) for u in range(2)]
+        w1_words = keep.tile([P, H], U32, name="w1_words", align_bytes=64)
+        w1_scales = keep.tile([P, H], U8, name="w1_scales", align_bytes=64)
+        dealt = w1_raw[:].rearrange("p (j m u e) -> p u m j e", j=PACK, u=2, e=2)
+        for u, m0, m1, copy in ((0, 0, P, nc.scalar.copy), (1, 0, SHARE, nc.scalar.copy), (1, SHARE, P, nc.vector.tensor_copy)):
+            copy(w1_bf[u][:, :, m0:m1, :].rearrange("p e m j -> p m j e"), dealt[:, u, m0:m1])
+        for u in range(2):
             cols = slice(2 * P * u, 2 * P * (u + 1))
-            nc.vector.quantize_mx(out=w1c[:, cols].bitcast(FP8X4), scales=w1s[:, cols], in_=w1_bf[u][:].rearrange("p e m j -> p (e m j)"))
-        w2w = reuse.tile([P, N], U32, name="w2w", align_bytes=64, offset=2048 + 128)
+            nc.vector.quantize_mx(out=w1_words[:, cols].bitcast(FP8X4), scales=w1_scales[:, cols], in_=w1_bf[u][:].rearrange("p e m j -> p (e m j)"))
+
+        w2w = reuse.tile([P, N], U32, name="w2w", align_bytes=64, offset=pair_bytes + N)
         nc.sync.dma_start(w2w[:].bitcast(I32), w2_words[0].rearrange("p n t -> p (n t)").bitcast(I32))
-        w2s = reuse.tile([P, N], U8, name="w2s", align_bytes=64, offset=2048)
+        w2s = reuse.tile([P, N], U8, name="w2s", align_bytes=64, offset=pair_bytes)
         for j in range(4):
             nc.sync.dma_start(w2s[:].bitcast(I32)[j:P:4, :], w2_scales[0].bitcast(I32)[j:16:4, :].unsqueeze(1).to_broadcast([4, 8, N // 4]))
-        if PEWARM:
-            wbank = ypsum.tile([P, V], F32, name="bank")
-            for codes, scales in ((onec[:, 0:32], picks[0][:, 0:32]), (onec[:, 0:32], picks[0][:, 0:32]),
-                                  (w1c[:, 0:32], w1s[:, 0:32]), (w1c[:, 2 * P : 2 * P + 32], w1s[:, 2 * P : 2 * P + 32])):
-                nc.tensor.matmul_mx(out=wbank[0:32, :], lhsT=codes.bitcast(FP8X4), lhsT_scale=scales,
-                                    rhs=onec[:].bitcast(FP8X4), rhs_scale=ones_s[:], start=True, stop=True)
 
-        piece = 2 * CH
-        xw_picked = {}
-        for i in GORDER:
-            xw_picked[i] = keep.tile([P, piece], U32, name="xw_picked%d" % i, align_bytes=64)
-            nc.vector.tensor_copy(xw_picked[i][:], xw[:].indirect(lists[:, piece // 16 * i : piece // 16 * (i + 1)]))
+        warm_bank = banks.tile([P, BANK], F32, name="bank")
+        early = (warm_words[:, 0:WARM_M], picked[0][:, 0:WARM_M])
+        late = [(w1_words[:, 2 * P * u : 2 * P * u + WARM_M], w1_scales[:, 2 * P * u : 2 * P * u + WARM_M]) for u in range(2)]
+        for words, scales in [early, early] + late:
+            nc.tensor.matmul_mx(out=warm_bank[0:WARM_M, :], lhsT=words.bitcast(FP8X4), lhsT_scale=scales,
+                                rhs=warm_words[:].bitcast(FP8X4), rhs_scale=warm_scales[:], start=True, stop=True)
 
-        def scale_of(col, n):
-            i = 0 if col < BYTE_PARTS[0][1] else 1
-            return placed[i][:, col - BYTE_PARTS[i][0] : col - BYTE_PARTS[i][0] + n]
+        pieces = {}
+        for v0 in range(0, V, PIECE):
+            for e0 in (v0, V + v0):
+                pieces[e0 // PIECE] = keep.tile([P, PIECE], U32, name="piece%d" % (e0 // PIECE), align_bytes=64)
+                nc.vector.tensor_copy(pieces[e0 // PIECE][:], xw[:].indirect(lists[:, e0 // LANES : (e0 + PIECE) // LANES]))
 
-        def first(dst, t, col, n=CH):
-            part = xw_picked[col // piece][:, col % piece : col % piece + n]
-            nc.tensor.matmul_mx(out=dst, lhsT=w1c[:, P * t : P * (t + 1)].bitcast(FP8X4), lhsT_scale=w1s[:, P * t : P * (t + 1)],
-                                rhs=part.bitcast(FP8X4), rhs_scale=scale_of(col, n), start=True, stop=True)
+        def product(dst, t, e0, n):
+            part = 0 if e0 < BYTE_GATHERS[1][0][0] else 1
+            s0 = e0 - BYTE_GATHERS[part][0][0]
+            nc.tensor.matmul_mx(out=dst, lhsT=w1_words[:, P * t : P * (t + 1)].bitcast(FP8X4), lhsT_scale=w1_scales[:, P * t : P * (t + 1)],
+                                rhs=pieces[e0 // PIECE][:, e0 % PIECE : e0 % PIECE + n].bitcast(FP8X4), rhs_scale=placed[part][:, s0 : s0 + n],
+                                start=True, stop=True)
 
-        zmax = {}
-        held = {}
-        zbf = keep.tile([P, V * PACK], BF16, name="zbf", align_bytes=64)
-        zm = [keep.tile([P, CH * PACK], F32, name="zm%d" % c, align_bytes=64) for c in range(NCH)]
-        res = [keep.tile([P, c1 - c0], F32, name="res%d" % i, align_bytes=64) for i, (c0, c1) in enumerate(STORES)]
-        HALF = CH // 2
+        z = keep.tile([P, V * PACK], BF16, name="z", align_bytes=64)
+        maxima = [keep.tile([P, CHUNK * PACK], F32, name="maxima%d" % c, align_bytes=64) for c in range(V // CHUNK)]
+        results = [keep.tile([P, STORE], F32, name="result%d" % i, align_bytes=64) for i in range(V // STORE)]
+        first_reads = {}
+        last = V // CHUNK - 1
 
-        def half(c, h):
-            bank = ypsum.tile([P, 2, PACK, HALF], F32, name="bank")
+        def first_read(c):
+            bank = banks.tile([P, PACK, CHUNK], F32, name="bank")
+            for t in range(PACK):
+                product(bank[:, t, :], t, CHUNK * c, CHUNK)
+            first_reads[c] = keep.tile([P, CHUNK, PACK], F32, name="first_read%d" % c, align_bytes=64)
+            nc.scalar.copy(first_reads[c][:], bank[:].rearrange("p t v -> p v t"))
+
+        def second_read(c):
+            bank = banks.tile([P, PACK, CHUNK], F32, name="bank")
+            for t in range(PACK):
+                product(bank[:, t, :], t, V + CHUNK * c, CHUNK)
+            nc.vector.tensor_tensor(maxima[c][:].rearrange("p (v t) -> p v t", t=PACK), bank[:].rearrange("p t v -> p v t"), first_reads[c][:], MAX)
+
+        def both_reads(h):
+            bank = banks.tile([P, 2, PACK, HALF], F32, name="bank")
             for t in range(PACK):
                 for r in range(2):
-                    first(bank[:, r, t, :], t, V * r + CH * c + HALF * h, HALF)
-            nc.vector.tensor_reduce(zm[c][:, PACK * HALF * h : PACK * HALF * (h + 1)].rearrange("p (v t) -> p v t", t=PACK),
-                                    bank[:].rearrange("p r t v -> p v t r"), AX, MAX)
+                    product(bank[:, r, t, :], t, V * r + CHUNK * last + HALF * h, HALF)
+            for v0, v1 in LAST_PIECES[h]:
+                nc.vector.tensor_reduce(maxima[last][:, PACK * (HALF * h + v0) : PACK * (HALF * h + v1)].rearrange("p (v t) -> p v t", t=PACK),
+                                        bank[:, :, :, v0:v1].rearrange("p r t v -> p v t r"), AXIS_X, MAX)
 
-        def copied_half(c, h):
-            bank = ypsum.tile([P, 2, PACK, HALF], F32, name="bank")
-            for r in range(2):
-                for t in range(PACK):
-                    first(bank[:, r, t, :], t, V * r + CH * c + HALF * h, HALF)
-            ya = work.tile([P, HALF, PACK], F32, name="yq", align_bytes=64)
-            nc.scalar.copy(ya[:], bank[:, 0].rearrange("p t v -> p v t"))
-            nc.vector.tensor_tensor(zm[c][:, PACK * HALF * h : PACK * HALF * (h + 1)].rearrange("p (v t) -> p v t", t=PACK),
-                                    bank[:, 1].rearrange("p t v -> p v t"), ya[:], MAX)
+        def gelu(c, v0, v1):
+            nc.scalar.activation(z[:, PACK * (CHUNK * c + v0) : PACK * (CHUNK * c + v1)], maxima[c][:, PACK * v0 : PACK * v1], GELU, bias=bias[:])
 
-        def read_a_split(c):
-            ya = work.tile([P, CH, PACK], F32, name="ya", align_bytes=64)
-            for u in range(2):
-                bank_a = ypsum.tile([P, 2, CH], F32, name="bank")
-                for e in range(2):
-                    first(bank_a[:, e, :], 2 * u + e, CH * c)
-                nc.scalar.copy(ya[:, :, 2 * u : 2 * u + 2], bank_a[:].rearrange("p e v -> p v e"))
-            held[c] = ya
+        first_read(0)
+        first_read(1)
+        second_read(0)
+        second_read(1)
+        first_read(2)
+        gelu(0, 0, CHUNK)
+        second_read(2)
+        gelu(1, 0, CHUNK)
+        both_reads(0)
+        both_reads(1)
+        gelu(2, 0, CHUNK)
+        for h in range(2):
+            for v0, v1 in LAST_PIECES[h]:
+                gelu(last, HALF * h + v0, HALF * h + v1)
 
-        def activate_half(c, h):
-            v0 = CH * c + HALF * h
-            nc.scalar.activation(zbf[:, PACK * v0 : PACK * (v0 + HALF)], zm[c][:, PACK * HALF * h : PACK * HALF * (h + 1)], GELU, bias=warm[:])
-
-        def both(c, u):
-            bank = ypsum.tile([P, 2, 2, CH], F32, name="bank")
-            for e in range(2):
-                for r in range(2):
-                    first(bank[:, r, e, :], 2 * u + e, V * r + CH * c)
-            nc.vector.tensor_reduce(zm[c][:, 2 * CH * u : 2 * CH * (u + 1)].rearrange("p (v e) -> p v e", e=2),
-                                    bank[:].rearrange("p r e v -> p v e r"), AX, MAX)
-            zmax[c] = zm[c][:].rearrange("p (u v e) -> p v u e", u=2, e=2)
-
-        def pair(c, u):
-            bank = ypsum.tile([P, 2, 2, CH], F32, name="bank")
-            for e in range(2):
-                for r in range(2):
-                    first(bank[:, r, e, :], 2 * u + e, V * r + CH * c)
-            ya = work.tile([P, CH, 2], F32, name="yh", align_bytes=64)
-            nc.scalar.copy(ya[:], bank[:, 0].rearrange("p e v -> p v e"))
-            nc.vector.tensor_tensor(zm[c][:, 2 * CH * u : 2 * CH * (u + 1)].rearrange("p (v e) -> p v e", e=2), bank[:, 1].rearrange("p e v -> p v e"), ya[:], MAX)
-            zmax[c] = zm[c][:].rearrange("p (u v e) -> p v u e", u=2, e=2)
-
-        def read_a(c):
-            bank_a = ypsum.tile([P, 2, 2, CH], F32, name="bank")
-            for t in range(PACK):
-                first(bank_a[:, t // 2, t % 2, :], t, CH * c)
-            ya = work.tile([P, CH, PACK], F32, name="ya", align_bytes=64)
-            nc.scalar.copy(ya[:], bank_a[:].rearrange("p u e v -> p v (u e)"))
-            held[c] = ya
-
-        def read_b(c):
-            bank_b = ypsum.tile([P, 2, 2, CH], F32, name="bank")
-            for t in range(PACK):
-                first(bank_b[:, t // 2, t % 2, :], t, V + CH * c)
-            nc.vector.tensor_tensor(zm[c][:].rearrange("p (v t) -> p v t", t=PACK), bank_b[:].rearrange("p u e v -> p v (u e)"), held[c][:], MAX)
-            zmax[c] = zm[c][:].rearrange("p (v u e) -> p v u e", u=2, e=2)
-
-        def activate(c):
-            nc.scalar.activation(zbf[:, c * CH * PACK : (c + 1) * CH * PACK].rearrange("p (v u e) -> p v u e", u=2, e=2), zmax[c], GELU, bias=warm[:])
-
-        def second(g):
-            c0, c1 = GROUPS[g]
-            w = c1 - c0
-            zc = keep.tile([P, w], U32, name="zc%d" % g, align_bytes=64)
-            zs = keep.tile([P, w], U8, name="zs%d" % g, align_bytes=64)
-            nc.vector.quantize_mx(out=zc[:].bitcast(FP8X4), scales=zs[:], in_=zbf[:, PACK * c0 : PACK * c1])
-            acc = ypsum.tile([P, V], F32, name="bank")
-            nc.tensor.matmul_mx(out=acc[:, 0:w], lhsT=w2w[:].bitcast(FP8X4), lhsT_scale=w2s[:], rhs=zc[:].bitcast(FP8X4), rhs_scale=zs[:], start=True, stop=True)
-            held["acc", g] = acc
-
-        def leave(g):
-            c0, c1 = GROUPS[g]
-            i = [k for k, (s0, s1) in enumerate(STORES) if s0 <= c0 < s1][0]
-            s0, s1 = STORES[i]
-            if g in OUT_ON_SCALAR:
-                nc.scalar.copy(res[i][:, c0 - s0 : c1 - s0], held["acc", g][:, 0 : c1 - c0])
-            else:
-                nc.vector.tensor_copy(res[i][:, c0 - s0 : c1 - s0], held["acc", g][:, 0 : c1 - c0])
-            if c1 == s1:
-                queue = nc.sync
-                queue.dma_start(out[:, s0:s1], res[i][:])
-
-        for word in ORDER.split():
-            kind, c = word[0], int(word[1])
-            if kind == "a":
-                read_a(c)
-            elif kind == "b":
-                read_b(c)
-            elif kind == "u":
-                both(c, 0)
-            elif kind == "v":
-                both(c, 1)
-            elif kind == "p":
-                pair(c, 0)
-            elif kind == "r":
-                pair(c, 1)
-            elif kind == "h":
-                half(c, int(word[2]))
-            elif kind == "c":
-                copied_half(c, int(word[2]))
-            elif kind == "s":
-                read_a_split(c)
-            elif kind == "k":
-                activate_half(c, int(word[2]))
-            elif kind == "g":
-                activate(c)
-            elif kind == "q":
-                second(c)
-            else:
-                leave(c)
+        sums = []
+        for g, (v0, v1) in enumerate(GROUPS):
+            z_words = keep.tile([P, v1 - v0], U32, name="z_words%d" % g, align_bytes=64)
+            z_scales = keep.tile([P, v1 - v0], U8, name="z_scales%d" % g, align_bytes=64)
+            nc.vector.quantize_mx(out=z_words[:].bitcast(FP8X4), scales=z_scales[:], in_=z[:, PACK * v0 : PACK * v1])
+            sums.append(banks.tile([P, BANK], F32, name="bank"))
+            nc.tensor.matmul_mx(out=sums[g][:, 0 : v1 - v0], lhsT=w2w[:].bitcast(FP8X4), lhsT_scale=w2s[:],
+                                rhs=z_words[:].bitcast(FP8X4), rhs_scale=z_scales[:], start=True, stop=True)
+        for g, (v0, v1) in enumerate(GROUPS):
+            i = v0 // STORE
+            copy = nc.scalar.copy if g < GROUPS_ON_SCALAR else nc.vector.tensor_copy
+            copy(results[i][:, v0 - STORE * i : v1 - STORE * i], sums[g][:, 0 : v1 - v0])
+            if v1 % STORE == 0:
+                nc.sync.dma_start(out[:, STORE * i : STORE * (i + 1)], results[i][:])

@@ -21,7 +21,7 @@ PACK = 4
 LANES = 16
 BANK = 512
 
-LEAD = 704
+LEAD = 576
 SHARE = 32
 BYTE_GATHERS = (((0, 512), (512, 768)), ((768, S),))
 PIECE = 256
@@ -46,20 +46,26 @@ def tile_picked_phpool_gelu_p_kernel(tc, x_words, x_scales, w1, w2_words, w2_sca
         w1_raw = keep.tile([P, PACK * H], F32, name="w1_raw", align_bytes=64)
         xs = keep.tile([P, T], U8, name="xs", align_bytes=64)
         nc.vector.memset(xs[:].bitcast(I32), 0)
-        nc.sync.dma_start(w1_raw[:, 0:LEAD], w1_rows[:, 0:LEAD])
+        w2w = keep.tile([P, BANK], U32, name="w2w", align_bytes=64)
+        nc.sync.dma_start(w2w[:, 0:N].bitcast(I32), w2_words[0].rearrange("p n t -> p (n t)").bitcast(I32))
         nc.sync.dma_start(lists[:], offs)
+        nc.sync.dma_start(w1_raw[:, 0:LEAD], w1_rows[:, 0:LEAD])
         nc.sync.dma_start(xs[:].bitcast(I32)[0:P:8, :], x_scales[0].bitcast(I32))
         nc.sync.dma_start(w1_raw[:, LEAD:], w1_rows[:, LEAD:])
+        w2s = keep.tile([P, BANK], U8, name="w2s", align_bytes=64)
+        nc.vector.memset(w2s[:].bitcast(I32), 0)
+        for j in range(4):
+            nc.sync.dma_start(w2s[:].bitcast(I32)[j:P:32, :].rearrange("p (r n) -> p r n", r=BANK // N),
+                              w2_scales[0].bitcast(I32)[j:16:4, :].unsqueeze(1).to_broadcast([4, BANK // N, N // 4]))
         xw = keep.tile([P, T], U32, name="xw", align_bytes=64)
         nc.sync.dma_start(xw[:].bitcast(I32), x_words[0].rearrange("p n t -> p (n t)").bitcast(I32))
 
-        zeros = keep.tile([P, PACK * BANK], BF16, name="zeros", align_bytes=64)
-        nc.vector.memset(zeros[:].bitcast(I32), 0)
+        zeros = keep.tile([P, 2], F32, name="zeros")
+        nc.vector.memset(zeros[:], 0.0)
         bias = keep.tile([P, 1], F32, name="bias")
         nc.scalar.activation(bias[:], zeros[:, 0:1], GELU)
-        warm_words = keep.tile([P, BANK], U32, name="warm_words", align_bytes=64)
-        warm_scales = keep.tile([P, BANK], U8, name="warm_scales", align_bytes=64)
-        nc.vector.quantize_mx(out=warm_words[:].bitcast(FP8X4), scales=warm_scales[:], in_=zeros[:])
+        nc.vector.tensor_copy(w2w[:, N:].bitcast(I32).rearrange("p (r n) -> p r n", n=N),
+                              w2w[:, 0:N].bitcast(I32).unsqueeze(1).to_broadcast([P, BANK // N - 1, N]))
 
         placed = []
         for part, gathers in enumerate(BYTE_GATHERS):
@@ -85,18 +91,12 @@ def tile_picked_phpool_gelu_p_kernel(tc, x_words, x_scales, w1, w2_words, w2_sca
             cols = slice(2 * P * u, 2 * P * (u + 1))
             nc.vector.quantize_mx(out=w1_words[:, cols].bitcast(FP8X4), scales=w1_scales[:, cols], in_=w1_bf[u][:].rearrange("p e m j -> p (e m j)"))
 
-        w2w = reuse.tile([P, N], U32, name="w2w", align_bytes=64, offset=pair_bytes + N)
-        nc.sync.dma_start(w2w[:].bitcast(I32), w2_words[0].rearrange("p n t -> p (n t)").bitcast(I32))
-        w2s = reuse.tile([P, N], U8, name="w2s", align_bytes=64, offset=pair_bytes)
-        for j in range(4):
-            nc.sync.dma_start(w2s[:].bitcast(I32)[j:P:4, :], w2_scales[0].bitcast(I32)[j:16:4, :].unsqueeze(1).to_broadcast([4, 8, N // 4]))
-
         warm_bank = banks.tile([P, BANK], F32, name="bank")
-        early = (warm_words[:, 0:WARM_M], picked[0][:, 0:WARM_M])
+        early = (w2w[:, 0:WARM_M], w2s[:, 0:WARM_M])
         late = [(w1_words[:, 2 * P * u : 2 * P * u + WARM_M], w1_scales[:, 2 * P * u : 2 * P * u + WARM_M]) for u in range(2)]
         for words, scales in [early, early] + late:
             nc.tensor.matmul_mx(out=warm_bank[0:WARM_M, :], lhsT=words.bitcast(FP8X4), lhsT_scale=scales,
-                                rhs=warm_words[:].bitcast(FP8X4), rhs_scale=warm_scales[:], start=True, stop=True)
+                                rhs=w2w[:].bitcast(FP8X4), rhs_scale=w2s[:], start=True, stop=True)
 
         pieces = {}
         for v0 in range(0, V, PIECE):
@@ -163,7 +163,7 @@ def tile_picked_phpool_gelu_p_kernel(tc, x_words, x_scales, w1, w2_words, w2_sca
             z_scales = keep.tile([P, v1 - v0], U8, name="z_scales%d" % g, align_bytes=64)
             nc.vector.quantize_mx(out=z_words[:].bitcast(FP8X4), scales=z_scales[:], in_=z[:, PACK * v0 : PACK * v1])
             sums.append(banks.tile([P, BANK], F32, name="bank"))
-            nc.tensor.matmul_mx(out=sums[g][:, 0 : v1 - v0], lhsT=w2w[:].bitcast(FP8X4), lhsT_scale=w2s[:],
+            nc.tensor.matmul_mx(out=sums[g][:, 0 : v1 - v0], lhsT=w2w[:, 0:N].bitcast(FP8X4), lhsT_scale=w2s[:, 0:N],
                                 rhs=z_words[:].bitcast(FP8X4), rhs_scale=z_scales[:], start=True, stop=True)
         for g, (v0, v1) in enumerate(GROUPS):
             i = v0 // STORE

@@ -21,9 +21,9 @@ PACK = 4
 LANES = 16
 BANK = 512
 
-LEAD = 576
+LEAD = 640
 SHARE = 32
-BYTE_GATHERS = (((0, 512), (512, 768)), ((768, S),))
+BYTE_GATHERS = (((0, 768),), ((768, S),))
 PIECE = 256
 CHUNK = 128
 HALF = 64
@@ -46,10 +46,13 @@ def tile_picked_phpool_gelu_p_kernel(tc, x_words, x_scales, w1, w2_words, w2_sca
         w1_raw = keep.tile([P, PACK * H], F32, name="w1_raw", align_bytes=64)
         xs = keep.tile([P, T], U8, name="xs", align_bytes=64)
         nc.vector.memset(xs[:].bitcast(I32), 0)
-        w2w = keep.tile([P, BANK], U32, name="w2w", align_bytes=64)
-        nc.sync.dma_start(w2w[:, 0:N].bitcast(I32), w2_words[0].rearrange("p n t -> p (n t)").bitcast(I32))
-        nc.sync.dma_start(lists[:], offs)
+        w2_first = keep.tile([P, WARM_M], U32, name="w2_first", align_bytes=64)
+        w2w = keep.tile([P, N], U32, name="w2w", align_bytes=64)
+        warm_words = keep.tile([P, BANK], U32, name="warm_words", align_bytes=64)
+        w2_rows = w2_words[0].rearrange("p n t -> p (n t)").bitcast(I32)
+        nc.sync.dma_start(w2_first[:].bitcast(I32), w2_rows[:, 0:WARM_M])
         nc.sync.dma_start(w1_raw[:, 0:LEAD], w1_rows[:, 0:LEAD])
+        nc.sync.dma_start(lists[:], offs)
         nc.sync.dma_start(xs[:].bitcast(I32)[0:P:8, :], x_scales[0].bitcast(I32))
         nc.sync.dma_start(w1_raw[:, LEAD:], w1_rows[:, LEAD:])
         w2s = keep.tile([P, BANK], U8, name="w2s", align_bytes=64)
@@ -59,13 +62,15 @@ def tile_picked_phpool_gelu_p_kernel(tc, x_words, x_scales, w1, w2_words, w2_sca
                               w2_scales[0].bitcast(I32)[j:16:4, :].unsqueeze(1).to_broadcast([4, BANK // N, N // 4]))
         xw = keep.tile([P, T], U32, name="xw", align_bytes=64)
         nc.sync.dma_start(xw[:].bitcast(I32), x_words[0].rearrange("p n t -> p (n t)").bitcast(I32))
+        nc.sync.dma_start(w2w[:, WARM_M:].bitcast(I32), w2_rows[:, WARM_M:])
 
         zeros = keep.tile([P, 2], F32, name="zeros")
         nc.vector.memset(zeros[:], 0.0)
         bias = keep.tile([P, 1], F32, name="bias")
         nc.scalar.activation(bias[:], zeros[:, 0:1], GELU)
-        nc.vector.tensor_copy(w2w[:, N:].bitcast(I32).rearrange("p (r n) -> p r n", n=N),
-                              w2w[:, 0:N].bitcast(I32).unsqueeze(1).to_broadcast([P, BANK // N - 1, N]))
+        nc.vector.tensor_copy(w2w[:, 0:WARM_M].bitcast(I32), w2_first[:].bitcast(I32))
+        nc.vector.tensor_copy(warm_words[:].bitcast(I32).rearrange("p (r n) -> p r n", n=WARM_M),
+                              w2_first[:].bitcast(I32).unsqueeze(1).to_broadcast([P, BANK // WARM_M, WARM_M]))
 
         placed = []
         for part, gathers in enumerate(BYTE_GATHERS):
@@ -92,11 +97,11 @@ def tile_picked_phpool_gelu_p_kernel(tc, x_words, x_scales, w1, w2_words, w2_sca
             nc.vector.quantize_mx(out=w1_words[:, cols].bitcast(FP8X4), scales=w1_scales[:, cols], in_=w1_bf[u][:].rearrange("p e m j -> p (e m j)"))
 
         warm_bank = banks.tile([P, BANK], F32, name="bank")
-        early = (w2w[:, 0:WARM_M], w2s[:, 0:WARM_M])
+        early = (w2_first[:], w2s[:, 0:WARM_M])
         late = [(w1_words[:, 2 * P * u : 2 * P * u + WARM_M], w1_scales[:, 2 * P * u : 2 * P * u + WARM_M]) for u in range(2)]
         for words, scales in [early, early] + late:
             nc.tensor.matmul_mx(out=warm_bank[0:WARM_M, :], lhsT=words.bitcast(FP8X4), lhsT_scale=scales,
-                                rhs=w2w[:].bitcast(FP8X4), rhs_scale=w2s[:], start=True, stop=True)
+                                rhs=warm_words[:].bitcast(FP8X4), rhs_scale=w2s[:], start=True, stop=True)
 
         pieces = {}
         for v0 in range(0, V, PIECE):
@@ -163,7 +168,7 @@ def tile_picked_phpool_gelu_p_kernel(tc, x_words, x_scales, w1, w2_words, w2_sca
             z_scales = keep.tile([P, v1 - v0], U8, name="z_scales%d" % g, align_bytes=64)
             nc.vector.quantize_mx(out=z_words[:].bitcast(FP8X4), scales=z_scales[:], in_=z[:, PACK * v0 : PACK * v1])
             sums.append(banks.tile([P, BANK], F32, name="bank"))
-            nc.tensor.matmul_mx(out=sums[g][:, 0 : v1 - v0], lhsT=w2w[:, 0:N].bitcast(FP8X4), lhsT_scale=w2s[:, 0:N],
+            nc.tensor.matmul_mx(out=sums[g][:, 0 : v1 - v0], lhsT=w2w[:].bitcast(FP8X4), lhsT_scale=w2s[:, 0:N],
                                 rhs=z_words[:].bitcast(FP8X4), rhs_scale=z_scales[:], start=True, stop=True)
         for g, (v0, v1) in enumerate(GROUPS):
             i = v0 // STORE

@@ -21,9 +21,9 @@ PACK = 4
 LANES = 16
 BANK = 512
 
-LEAD = 640
 SHARE = 32
-BYTE_GATHERS = (((0, 768),), ((768, S),))
+CLEAR = 1216
+BYTE_PARTS = ((0, 768), (768, S))
 PIECE = 256
 CHUNK = 128
 HALF = 64
@@ -32,6 +32,7 @@ GROUPS = ((0, 128), (128, 256), (256, 384), (384, 448), (448, 512))
 STORE = 128
 GROUPS_ON_SCALAR = 2
 WARM_M = 32
+WARM_N = (512, 512, 512, 128, 128)
 
 
 def tile_picked_phpool_gelu_p_kernel(tc, x_words, x_scales, w1, w2_words, w2_scales, offs, out):
@@ -42,66 +43,67 @@ def tile_picked_phpool_gelu_p_kernel(tc, x_words, x_scales, w1, w2_words, w2_sca
         banks = ctx.enter_context(tc.psum_pool(name="banks", bufs=8))
 
         lists = keep.tile([P, S // LANES], U16, name="lists")
-        w1_rows = w1.rearrange("(p j) c -> p (j c)", j=PACK)
-        w1_raw = keep.tile([P, PACK * H], F32, name="w1_raw", align_bytes=64)
+        w1_rows = w1.rearrange("(p j) c -> p j c", j=PACK)
+        w1_raw = [keep.tile([P, PACK, H // 2], F32, name="w1_raw%d" % h, align_bytes=64) for h in range(2)]
         xs = keep.tile([P, T], U8, name="xs", align_bytes=64)
-        nc.vector.memset(xs[:].bitcast(I32), 0)
+        nc.vector.memset(xs[:, 0:CLEAR].bitcast(I32), 0)
+        nc.gpsimd.memset(xs[:, CLEAR:].bitcast(I32), 0)
         w2_first = keep.tile([P, WARM_M], U32, name="w2_first", align_bytes=64)
-        w2w = keep.tile([P, N], U32, name="w2w", align_bytes=64)
-        warm_words = keep.tile([P, BANK], U32, name="warm_words", align_bytes=64)
         w2_rows = w2_words[0].rearrange("p n t -> p (n t)").bitcast(I32)
-        nc.sync.dma_start(w2_first[:].bitcast(I32), w2_rows[:, 0:WARM_M])
-        nc.sync.dma_start(w1_raw[:, 0:LEAD], w1_rows[:, 0:LEAD])
+        w2_spread = reuse.tile([P, N], U8, name="w2_spread", align_bytes=64, offset=0)
+        nc.sync.dma_start(w1_raw[0][:, 0:2, :], w1_rows[:, 0:2, 0 : H // 2])
         nc.sync.dma_start(lists[:], offs)
+        nc.sync.dma_start(w2_first[:].bitcast(I32), w2_rows[:, 0:WARM_M])
         nc.sync.dma_start(xs[:].bitcast(I32)[0:P:8, :], x_scales[0].bitcast(I32))
-        nc.sync.dma_start(w1_raw[:, LEAD:], w1_rows[:, LEAD:])
-        w2s = keep.tile([P, BANK], U8, name="w2s", align_bytes=64)
-        nc.vector.memset(w2s[:].bitcast(I32), 0)
-        for j in range(4):
-            nc.sync.dma_start(w2s[:].bitcast(I32)[j:P:32, :].rearrange("p (r n) -> p r n", r=BANK // N),
-                              w2_scales[0].bitcast(I32)[j:16:4, :].unsqueeze(1).to_broadcast([4, BANK // N, N // 4]))
+        nc.sync.dma_start(w2_spread[:].bitcast(I32), w2_scales[0].bitcast(I32).unsqueeze(1).to_broadcast([16, 8, N // 4]))
+        nc.sync.dma_start(w1_raw[0][:, 2:, :], w1_rows[:, 2:, 0 : H // 2])
+        nc.sync.dma_start(w1_raw[1][:], w1_rows[:, :, H // 2 :])
         xw = keep.tile([P, T], U32, name="xw", align_bytes=64)
         nc.sync.dma_start(xw[:].bitcast(I32), x_words[0].rearrange("p n t -> p (n t)").bitcast(I32))
-        nc.sync.dma_start(w2w[:, WARM_M:].bitcast(I32), w2_rows[:, WARM_M:])
 
-        zeros = keep.tile([P, 2], F32, name="zeros")
-        nc.vector.memset(zeros[:], 0.0)
+        zero = keep.tile([P, 1], F32, name="zero")
+        nc.vector.memset(zero[:], 0.0)
         bias = keep.tile([P, 1], F32, name="bias")
-        nc.scalar.activation(bias[:], zeros[:, 0:1], GELU)
-        nc.vector.tensor_copy(w2w[:, 0:WARM_M].bitcast(I32), w2_first[:].bitcast(I32))
-        nc.vector.tensor_copy(warm_words[:].bitcast(I32).rearrange("p (r n) -> p r n", n=WARM_M),
-                              w2_first[:].bitcast(I32).unsqueeze(1).to_broadcast([P, BANK // WARM_M, WARM_M]))
+        nc.scalar.activation(bias[:], zero[:], GELU)
+        w2w = keep.tile([P, BANK], U32, name="w2w", align_bytes=64)
+        nc.scalar.copy(w2w[:].rearrange("p (r n) -> p r n", n=WARM_M), w2_first[:].unsqueeze(1).to_broadcast([P, BANK // WARM_M, WARM_M]))
 
         placed = []
-        for part, gathers in enumerate(BYTE_GATHERS):
-            placed.append(keep.tile([P, gathers[-1][1] - gathers[0][0]], U8, name="placed%d" % part, align_bytes=64))
-            nc.vector.memset(placed[part][:].bitcast(I32), 0)
-        picked = []
-        for part, gathers in enumerate(BYTE_GATHERS):
-            base = gathers[0][0]
-            picked.append(keep.tile([P, gathers[-1][1] - base], U8, name="picked%d" % part, align_bytes=64))
-            for e0, e1 in gathers:
-                nc.vector.tensor_copy(picked[part][:, e0 - base : e1 - base], xs[:].indirect(lists[:, e0 // LANES : e1 // LANES]))
-            for j in range(4):
-                nc.sync.dma_start(placed[part][:].bitcast(I32)[j:P:32, :], picked[part][:].bitcast(I32)[8 * j : P : 32, :])
+        for part, (e0, e1) in enumerate(BYTE_PARTS):
+            placed.append(keep.tile([P, e1 - e0], U8, name="placed%d" % part, align_bytes=64))
+            nc.gpsimd.memset(placed[part][:].bitcast(I32), 0)
 
-        pair_bytes = 2 * P * PACK * 2
-        w1_bf = [reuse.tile([P, 2, P, PACK], BF16, name="w1_bf%d" % u, align_bytes=64, offset=pair_bytes * u) for u in range(2)]
+        def pick_bytes(part, picked):
+            e0, e1 = BYTE_PARTS[part]
+            nc.vector.tensor_copy(picked[:], xs[:].indirect(lists[:, e0 // LANES : e1 // LANES]))
+            for j in range(4):
+                nc.sync.dma_start(placed[part][:].bitcast(I32)[j:P:32, :], picked[:].bitcast(I32)[8 * j : P : 32, :])
+
+        pick_bytes(0, keep.tile([P, BYTE_PARTS[0][1]], U8, name="picked0", align_bytes=64))
+        w2s = keep.tile([P, BANK], U8, name="w2s", align_bytes=64)
+        nc.vector.tensor_copy(w2s[:].bitcast(I32).rearrange("p (r n) -> p r n", n=N // 4),
+                              w2_spread[:].bitcast(I32).unsqueeze(1).to_broadcast([P, BANK // N, N // 4]))
+        pick_bytes(1, reuse.tile([P, S - BYTE_PARTS[1][0]], U8, name="picked1", align_bytes=64, offset=0))
+
+        warm_bank = banks.tile([P, BANK], F32, name="bank")
+        for n in WARM_N:
+            nc.tensor.matmul_mx(out=warm_bank[0:WARM_M, 0:n], lhsT=w2w[:, 0:WARM_M].bitcast(FP8X4), lhsT_scale=w2s[:, 0:WARM_M],
+                                rhs=w2w[:, 0:n].bitcast(FP8X4), rhs_scale=w2s[:, 0:n], start=True, stop=True)
+        nc.sync.dma_start(w2w[:, WARM_M:N].bitcast(I32), w2_rows[:, WARM_M:])
+        for j in range(1, 4):
+            nc.sync.dma_start(w2s[:, 0:N].bitcast(I32)[j:P:32, :], w2_scales[0].bitcast(I32)[j:16:4, :])
+
+        w1_bf = [keep.tile([P, 2, P, PACK], BF16, name="w1_bf%d" % u, align_bytes=64) for u in range(2)]
         w1_words = keep.tile([P, H], U32, name="w1_words", align_bytes=64)
         w1_scales = keep.tile([P, H], U8, name="w1_scales", align_bytes=64)
-        dealt = w1_raw[:].rearrange("p (j m u e) -> p u m j e", j=PACK, u=2, e=2)
-        for u, m0, m1, copy in ((0, 0, P, nc.scalar.copy), (1, 0, SHARE, nc.scalar.copy), (1, SHARE, P, nc.vector.tensor_copy)):
-            copy(w1_bf[u][:, :, m0:m1, :].rearrange("p e m j -> p m j e"), dealt[:, u, m0:m1])
+        dealt = [w1_raw[h][:].rearrange("p j (m u e) -> p u m j e", u=2, e=2) for h in range(2)]
+        half = P // 2
+        for h, u, m0, m1, copy in ((0, 0, 0, half, nc.scalar.copy), (0, 1, 0, half, nc.scalar.copy), (1, 0, 0, half, nc.scalar.copy),
+                                   (1, 1, 0, SHARE, nc.scalar.copy), (1, 1, SHARE, half, nc.vector.tensor_copy)):
+            copy(w1_bf[u][:, :, half * h + m0 : half * h + m1, :].rearrange("p e m j -> p m j e"), dealt[h][:, u, m0:m1])
         for u in range(2):
             cols = slice(2 * P * u, 2 * P * (u + 1))
             nc.vector.quantize_mx(out=w1_words[:, cols].bitcast(FP8X4), scales=w1_scales[:, cols], in_=w1_bf[u][:].rearrange("p e m j -> p (e m j)"))
-
-        warm_bank = banks.tile([P, BANK], F32, name="bank")
-        early = (w2_first[:], w2s[:, 0:WARM_M])
-        late = [(w1_words[:, 2 * P * u : 2 * P * u + WARM_M], w1_scales[:, 2 * P * u : 2 * P * u + WARM_M]) for u in range(2)]
-        for words, scales in [early, early] + late:
-            nc.tensor.matmul_mx(out=warm_bank[0:WARM_M, :], lhsT=words.bitcast(FP8X4), lhsT_scale=scales,
-                                rhs=warm_words[:].bitcast(FP8X4), rhs_scale=w2s[:], start=True, stop=True)
 
         pieces = {}
         for v0 in range(0, V, PIECE):
@@ -110,8 +112,8 @@ def tile_picked_phpool_gelu_p_kernel(tc, x_words, x_scales, w1, w2_words, w2_sca
                 nc.vector.tensor_copy(pieces[e0 // PIECE][:], xw[:].indirect(lists[:, e0 // LANES : (e0 + PIECE) // LANES]))
 
         def product(dst, t, e0, n):
-            part = 0 if e0 < BYTE_GATHERS[1][0][0] else 1
-            s0 = e0 - BYTE_GATHERS[part][0][0]
+            part = 0 if e0 < BYTE_PARTS[1][0] else 1
+            s0 = e0 - BYTE_PARTS[part][0]
             nc.tensor.matmul_mx(out=dst, lhsT=w1_words[:, P * t : P * (t + 1)].bitcast(FP8X4), lhsT_scale=w1_scales[:, P * t : P * (t + 1)],
                                 rhs=pieces[e0 // PIECE][:, e0 % PIECE : e0 % PIECE + n].bitcast(FP8X4), rhs_scale=placed[part][:, s0 : s0 + n],
                                 start=True, stop=True)
@@ -168,7 +170,7 @@ def tile_picked_phpool_gelu_p_kernel(tc, x_words, x_scales, w1, w2_words, w2_sca
             z_scales = keep.tile([P, v1 - v0], U8, name="z_scales%d" % g, align_bytes=64)
             nc.vector.quantize_mx(out=z_words[:].bitcast(FP8X4), scales=z_scales[:], in_=z[:, PACK * v0 : PACK * v1])
             sums.append(banks.tile([P, BANK], F32, name="bank"))
-            nc.tensor.matmul_mx(out=sums[g][:, 0 : v1 - v0], lhsT=w2w[:].bitcast(FP8X4), lhsT_scale=w2s[:, 0:N],
+            nc.tensor.matmul_mx(out=sums[g][:, 0 : v1 - v0], lhsT=w2w[:, 0:N].bitcast(FP8X4), lhsT_scale=w2s[:, 0:N],
                                 rhs=z_words[:].bitcast(FP8X4), rhs_scale=z_scales[:], start=True, stop=True)
         for g, (v0, v1) in enumerate(GROUPS):
             i = v0 // STORE

@@ -21,8 +21,8 @@ PACK = 4
 LANES = 16
 BANK = 512
 
+LEAD = 256
 SHARE = 32
-CLEAR = 1216
 BYTE_PARTS = ((0, 768), (768, S))
 PIECE = 256
 CHUNK = 128
@@ -43,21 +43,19 @@ def tile_picked_phpool_gelu_p_kernel(tc, x_words, x_scales, w1, w2_words, w2_sca
         banks = ctx.enter_context(tc.psum_pool(name="banks", bufs=8))
 
         lists = keep.tile([P, S // LANES], U16, name="lists")
-        w1_rows = w1.rearrange("(p j) c -> p j c", j=PACK)
-        w1_raw = [keep.tile([P, PACK, H // 2], F32, name="w1_raw%d" % h, align_bytes=64) for h in range(2)]
-        xs = keep.tile([P, T], U8, name="xs", align_bytes=64)
-        nc.vector.memset(xs[:, 0:CLEAR].bitcast(I32), 0)
-        nc.gpsimd.memset(xs[:, CLEAR:].bitcast(I32), 0)
+        w1_rows = w1.rearrange("(p j) c -> p (j c)", j=PACK)
+        w1_raw = keep.tile([P, PACK * H], F32, name="w1_raw", align_bytes=64)
+        xs = reuse.tile([P, T], U8, name="xs", align_bytes=64, offset=0)
+        nc.vector.memset(xs[:].bitcast(I32), 0)
         w2_first = keep.tile([P, WARM_M], U32, name="w2_first", align_bytes=64)
         w2_rows = w2_words[0].rearrange("p n t -> p (n t)").bitcast(I32)
-        w2_spread = reuse.tile([P, N], U8, name="w2_spread", align_bytes=64, offset=0)
-        nc.sync.dma_start(w1_raw[0][:, 0:2, :], w1_rows[:, 0:2, 0 : H // 2])
+        w2_spread = reuse.tile([P, N], U8, name="w2_spread", align_bytes=64, offset=T)
+        nc.sync.dma_start(w1_raw[:, 0:LEAD], w1_rows[:, 0:LEAD])
         nc.sync.dma_start(lists[:], offs)
         nc.sync.dma_start(w2_first[:].bitcast(I32), w2_rows[:, 0:WARM_M])
         nc.sync.dma_start(xs[:].bitcast(I32)[0:P:8, :], x_scales[0].bitcast(I32))
+        nc.sync.dma_start(w1_raw[:, LEAD:], w1_rows[:, LEAD:])
         nc.sync.dma_start(w2_spread[:].bitcast(I32), w2_scales[0].bitcast(I32).unsqueeze(1).to_broadcast([16, 8, N // 4]))
-        nc.sync.dma_start(w1_raw[0][:, 2:, :], w1_rows[:, 2:, 0 : H // 2])
-        nc.sync.dma_start(w1_raw[1][:], w1_rows[:, :, H // 2 :])
         xw = keep.tile([P, T], U32, name="xw", align_bytes=64)
         nc.sync.dma_start(xw[:].bitcast(I32), x_words[0].rearrange("p n t -> p (n t)").bitcast(I32))
 
@@ -71,19 +69,16 @@ def tile_picked_phpool_gelu_p_kernel(tc, x_words, x_scales, w1, w2_words, w2_sca
         placed = []
         for part, (e0, e1) in enumerate(BYTE_PARTS):
             placed.append(keep.tile([P, e1 - e0], U8, name="placed%d" % part, align_bytes=64))
-            nc.gpsimd.memset(placed[part][:].bitcast(I32), 0)
+            nc.vector.memset(placed[part][:].bitcast(I32), 0)
 
-        def pick_bytes(part, picked):
-            e0, e1 = BYTE_PARTS[part]
+        for part, (e0, e1) in enumerate(BYTE_PARTS):
+            picked = keep.tile([P, e1 - e0], U8, name="picked%d" % part, align_bytes=64)
             nc.vector.tensor_copy(picked[:], xs[:].indirect(lists[:, e0 // LANES : e1 // LANES]))
             for j in range(4):
                 nc.sync.dma_start(placed[part][:].bitcast(I32)[j:P:32, :], picked[:].bitcast(I32)[8 * j : P : 32, :])
-
-        pick_bytes(0, keep.tile([P, BYTE_PARTS[0][1]], U8, name="picked0", align_bytes=64))
-        w2s = keep.tile([P, BANK], U8, name="w2s", align_bytes=64)
+        w2s = reuse.tile([P, BANK], U8, name="w2s", align_bytes=64, offset=0)
         nc.vector.tensor_copy(w2s[:].bitcast(I32).rearrange("p (r n) -> p r n", n=N // 4),
                               w2_spread[:].bitcast(I32).unsqueeze(1).to_broadcast([P, BANK // N, N // 4]))
-        pick_bytes(1, reuse.tile([P, S - BYTE_PARTS[1][0]], U8, name="picked1", align_bytes=64, offset=0))
 
         warm_bank = banks.tile([P, BANK], F32, name="bank")
         for n in WARM_N:
@@ -93,14 +88,12 @@ def tile_picked_phpool_gelu_p_kernel(tc, x_words, x_scales, w1, w2_words, w2_sca
         for j in range(1, 4):
             nc.sync.dma_start(w2s[:, 0:N].bitcast(I32)[j:P:32, :], w2_scales[0].bitcast(I32)[j:16:4, :])
 
-        w1_bf = [keep.tile([P, 2, P, PACK], BF16, name="w1_bf%d" % u, align_bytes=64) for u in range(2)]
+        w1_bf = [keep.tile([P, 2, P, PACK], BF16, name="w1_bf0", align_bytes=64), reuse.tile([P, 2, P, PACK], BF16, name="w1_bf1", align_bytes=64, offset=T)]
         w1_words = keep.tile([P, H], U32, name="w1_words", align_bytes=64)
         w1_scales = keep.tile([P, H], U8, name="w1_scales", align_bytes=64)
-        dealt = [w1_raw[h][:].rearrange("p j (m u e) -> p u m j e", u=2, e=2) for h in range(2)]
-        half = P // 2
-        for h, u, m0, m1, copy in ((0, 0, 0, half, nc.scalar.copy), (0, 1, 0, half, nc.scalar.copy), (1, 0, 0, half, nc.scalar.copy),
-                                   (1, 1, 0, SHARE, nc.scalar.copy), (1, 1, SHARE, half, nc.vector.tensor_copy)):
-            copy(w1_bf[u][:, :, half * h + m0 : half * h + m1, :].rearrange("p e m j -> p m j e"), dealt[h][:, u, m0:m1])
+        dealt = w1_raw[:].rearrange("p (j m u e) -> p u m j e", j=PACK, u=2, e=2)
+        for u, m0, m1, copy in ((0, 0, P, nc.scalar.copy), (1, 0, SHARE, nc.scalar.copy), (1, SHARE, P, nc.vector.tensor_copy)):
+            copy(w1_bf[u][:, :, m0:m1, :].rearrange("p e m j -> p m j e"), dealt[:, u, m0:m1])
         for u in range(2):
             cols = slice(2 * P * u, 2 * P * (u + 1))
             nc.vector.quantize_mx(out=w1_words[:, cols].bitcast(FP8X4), scales=w1_scales[:, cols], in_=w1_bf[u][:].rearrange("p e m j -> p (e m j)"))

@@ -21,8 +21,7 @@ PACK = 4
 LANES = 16
 BANK = 512
 
-LEAD = 256
-SHARE = 32
+SHARE = 64
 BYTE_PARTS = ((0, 768), (768, S))
 PIECE = 256
 CHUNK = 128
@@ -39,23 +38,22 @@ def tile_picked_phpool_gelu_p_kernel(tc, x_words, x_scales, w1, w2_words, w2_sca
     nc = tc.nc
     with ExitStack() as ctx:
         keep = ctx.enter_context(tc.tile_pool(name="keep", bufs=1))
-        reuse = ctx.enter_context(tc.tile_pool(name="reuse", bufs=1))
         banks = ctx.enter_context(tc.psum_pool(name="banks", bufs=8))
 
         lists = keep.tile([P, S // LANES], U16, name="lists")
         w1_rows = w1.rearrange("(p j) c -> p (j c)", j=PACK)
         w1_raw = keep.tile([P, PACK * H], F32, name="w1_raw", align_bytes=64)
-        xs = reuse.tile([P, T], U8, name="xs", align_bytes=64, offset=0)
+        xs = keep.tile([P, T], U8, name="xs", align_bytes=64)
         nc.vector.memset(xs[:].bitcast(I32), 0)
         w2_first = keep.tile([P, WARM_M], U32, name="w2_first", align_bytes=64)
         w2_rows = w2_words[0].rearrange("p n t -> p (n t)").bitcast(I32)
-        w2_spread = reuse.tile([P, N], U8, name="w2_spread", align_bytes=64, offset=T)
-        nc.sync.dma_start(w1_raw[:, 0:LEAD], w1_rows[:, 0:LEAD])
+        w2_spread = keep.tile([P, N], U8, name="w2_spread", align_bytes=64)
+        nc.scalar.dma_start(w2_first[:].bitcast(I32), w2_rows[:, 0:WARM_M])
+        nc.scalar.dma_start(w2_spread[:].bitcast(I32), w2_scales[0].bitcast(I32).unsqueeze(1).to_broadcast([16, 8, N // 4]))
+        nc.sync.dma_start(w1_raw[:, 0:H], w1_rows[:, 0:H])
         nc.sync.dma_start(lists[:], offs)
-        nc.sync.dma_start(w2_first[:].bitcast(I32), w2_rows[:, 0:WARM_M])
         nc.sync.dma_start(xs[:].bitcast(I32)[0:P:8, :], x_scales[0].bitcast(I32))
-        nc.sync.dma_start(w1_raw[:, LEAD:], w1_rows[:, LEAD:])
-        nc.sync.dma_start(w2_spread[:].bitcast(I32), w2_scales[0].bitcast(I32).unsqueeze(1).to_broadcast([16, 8, N // 4]))
+        nc.sync.dma_start(w1_raw[:, H:], w1_rows[:, H:])
         xw = keep.tile([P, T], U32, name="xw", align_bytes=64)
         nc.sync.dma_start(xw[:].bitcast(I32), x_words[0].rearrange("p n t -> p (n t)").bitcast(I32))
 
@@ -76,27 +74,36 @@ def tile_picked_phpool_gelu_p_kernel(tc, x_words, x_scales, w1, w2_words, w2_sca
             nc.vector.tensor_copy(picked[:], xs[:].indirect(lists[:, e0 // LANES : e1 // LANES]))
             for j in range(4):
                 nc.sync.dma_start(placed[part][:].bitcast(I32)[j:P:32, :], picked[:].bitcast(I32)[8 * j : P : 32, :])
-        w2s = reuse.tile([P, BANK], U8, name="w2s", align_bytes=64, offset=0)
-        nc.vector.tensor_copy(w2s[:].bitcast(I32).rearrange("p (r n) -> p r n", n=N // 4),
-                              w2_spread[:].bitcast(I32).unsqueeze(1).to_broadcast([P, BANK // N, N // 4]))
+
+        w1_bf = [keep.tile([P, 2, P, PACK], BF16, name="w1_bf%d" % u, align_bytes=64) for u in range(2)]
+        w1_words = keep.tile([P, H], U32, name="w1_words", align_bytes=64)
+        w1_scales = keep.tile([P, H], U8, name="w1_scales", align_bytes=64)
+        dealt = w1_raw[:].rearrange("p (j m u e) -> p u m j e", j=PACK, u=2, e=2)
+
+        def round_w1(copy, u, m0, m1, j0, j1):
+            copy(w1_bf[u][:, :, m0:m1, j0:j1].rearrange("p e m j -> p m j e"), dealt[:, u, m0:m1, j0:j1])
+
+        round_w1(nc.scalar.copy, 0, 0, P, 0, 1)
+        round_w1(nc.scalar.copy, 1, 0, SHARE, 0, 1)
+        w2s = keep.tile([P, BANK], U8, name="w2s", align_bytes=64)
+        nc.scalar.copy(w2s[:].bitcast(U32).rearrange("p (r n) -> p r n", n=N // 4),
+                       w2_spread[:].bitcast(U32).unsqueeze(1).to_broadcast([P, BANK // N, N // 4]))
+        round_w1(nc.scalar.copy, 0, 0, P, 1, PACK)
+        round_w1(nc.scalar.copy, 1, 0, SHARE, 1, PACK)
+        round_w1(nc.vector.tensor_copy, 1, SHARE, P, 0, PACK)
+        for u in range(2):
+            cols = slice(2 * P * u, 2 * P * (u + 1))
+            nc.vector.quantize_mx(out=w1_words[:, cols].bitcast(FP8X4), scales=w1_scales[:, cols], in_=w1_bf[u][:].rearrange("p e m j -> p (e m j)"))
 
         warm_bank = banks.tile([P, BANK], F32, name="bank")
-        for n in WARM_N:
-            nc.tensor.matmul_mx(out=warm_bank[0:WARM_M, 0:n], lhsT=w2w[:, 0:WARM_M].bitcast(FP8X4), lhsT_scale=w2s[:, 0:WARM_M],
+        early = (w2w[:, 0:WARM_M], w2s[:, 0:WARM_M])
+        late = (w1_words[:, 0:WARM_M], w1_scales[:, 0:WARM_M])
+        for (words, scales), n in zip([early, early, early, late, late], WARM_N):
+            nc.tensor.matmul_mx(out=warm_bank[0:WARM_M, 0:n], lhsT=words.bitcast(FP8X4), lhsT_scale=scales,
                                 rhs=w2w[:, 0:n].bitcast(FP8X4), rhs_scale=w2s[:, 0:n], start=True, stop=True)
         nc.sync.dma_start(w2w[:, WARM_M:N].bitcast(I32), w2_rows[:, WARM_M:])
         for j in range(1, 4):
             nc.sync.dma_start(w2s[:, 0:N].bitcast(I32)[j:P:32, :], w2_scales[0].bitcast(I32)[j:16:4, :])
-
-        w1_bf = [keep.tile([P, 2, P, PACK], BF16, name="w1_bf0", align_bytes=64), reuse.tile([P, 2, P, PACK], BF16, name="w1_bf1", align_bytes=64, offset=T)]
-        w1_words = keep.tile([P, H], U32, name="w1_words", align_bytes=64)
-        w1_scales = keep.tile([P, H], U8, name="w1_scales", align_bytes=64)
-        dealt = w1_raw[:].rearrange("p (j m u e) -> p u m j e", j=PACK, u=2, e=2)
-        for u, m0, m1, copy in ((0, 0, P, nc.scalar.copy), (1, 0, SHARE, nc.scalar.copy), (1, SHARE, P, nc.vector.tensor_copy)):
-            copy(w1_bf[u][:, :, m0:m1, :].rearrange("p e m j -> p m j e"), dealt[:, u, m0:m1])
-        for u in range(2):
-            cols = slice(2 * P * u, 2 * P * (u + 1))
-            nc.vector.quantize_mx(out=w1_words[:, cols].bitcast(FP8X4), scales=w1_scales[:, cols], in_=w1_bf[u][:].rearrange("p e m j -> p (e m j)"))
 
         pieces = {}
         for v0 in range(0, V, PIECE):

@@ -21,7 +21,8 @@ PACK = 4
 LANES = 16
 BANK = 512
 
-SHARE = 64
+LEAD = 640
+SHARE = 80
 BYTE_PARTS = ((0, 768), (768, S))
 PIECE = 256
 CHUNK = 128
@@ -38,6 +39,7 @@ def tile_picked_phpool_gelu_p_kernel(tc, x_words, x_scales, w1, w2_words, w2_sca
     nc = tc.nc
     with ExitStack() as ctx:
         keep = ctx.enter_context(tc.tile_pool(name="keep", bufs=1))
+        reuse = ctx.enter_context(tc.tile_pool(name="reuse", bufs=1))
         banks = ctx.enter_context(tc.psum_pool(name="banks", bufs=8))
 
         lists = keep.tile([P, S // LANES], U16, name="lists")
@@ -47,13 +49,13 @@ def tile_picked_phpool_gelu_p_kernel(tc, x_words, x_scales, w1, w2_words, w2_sca
         nc.vector.memset(xs[:].bitcast(I32), 0)
         w2_first = keep.tile([P, WARM_M], U32, name="w2_first", align_bytes=64)
         w2_rows = w2_words[0].rearrange("p n t -> p (n t)").bitcast(I32)
-        w2_spread = keep.tile([P, N], U8, name="w2_spread", align_bytes=64)
+        w2_spread = reuse.tile([P, N], U8, name="w2_spread", align_bytes=64, offset=0)
         nc.scalar.dma_start(w2_first[:].bitcast(I32), w2_rows[:, 0:WARM_M])
-        nc.scalar.dma_start(w2_spread[:].bitcast(I32), w2_scales[0].bitcast(I32).unsqueeze(1).to_broadcast([16, 8, N // 4]))
-        nc.sync.dma_start(w1_raw[:, 0:H], w1_rows[:, 0:H])
+        nc.sync.dma_start(w1_raw[:, 0:LEAD], w1_rows[:, 0:LEAD])
         nc.sync.dma_start(lists[:], offs)
         nc.sync.dma_start(xs[:].bitcast(I32)[0:P:8, :], x_scales[0].bitcast(I32))
-        nc.sync.dma_start(w1_raw[:, H:], w1_rows[:, H:])
+        nc.sync.dma_start(w2_spread[:].bitcast(I32), w2_scales[0].bitcast(I32).unsqueeze(1).to_broadcast([16, 8, N // 4]))
+        nc.sync.dma_start(w1_raw[:, LEAD:], w1_rows[:, LEAD:])
         xw = keep.tile([P, T], U32, name="xw", align_bytes=64)
         nc.sync.dma_start(xw[:].bitcast(I32), x_words[0].rearrange("p n t -> p (n t)").bitcast(I32))
 
@@ -69,11 +71,17 @@ def tile_picked_phpool_gelu_p_kernel(tc, x_words, x_scales, w1, w2_words, w2_sca
             placed.append(keep.tile([P, e1 - e0], U8, name="placed%d" % part, align_bytes=64))
             nc.vector.memset(placed[part][:].bitcast(I32), 0)
 
-        for part, (e0, e1) in enumerate(BYTE_PARTS):
-            picked = keep.tile([P, e1 - e0], U8, name="picked%d" % part, align_bytes=64)
+        def pick_bytes(part, picked):
+            e0, e1 = BYTE_PARTS[part]
             nc.vector.tensor_copy(picked[:], xs[:].indirect(lists[:, e0 // LANES : e1 // LANES]))
             for j in range(4):
                 nc.sync.dma_start(placed[part][:].bitcast(I32)[j:P:32, :], picked[:].bitcast(I32)[8 * j : P : 32, :])
+
+        pick_bytes(0, keep.tile([P, BYTE_PARTS[0][1]], U8, name="picked0", align_bytes=64))
+        w2s = keep.tile([P, BANK], U8, name="w2s", align_bytes=64)
+        nc.vector.tensor_copy(w2s[:].bitcast(I32).rearrange("p (r n) -> p r n", n=N // 4),
+                              w2_spread[:].bitcast(I32).unsqueeze(1).to_broadcast([P, BANK // N, N // 4]))
+        pick_bytes(1, reuse.tile([P, S - BYTE_PARTS[1][0]], U8, name="picked1", align_bytes=64, offset=0))
 
         w1_bf = [keep.tile([P, 2, P, PACK], BF16, name="w1_bf%d" % u, align_bytes=64) for u in range(2)]
         w1_words = keep.tile([P, H], U32, name="w1_words", align_bytes=64)
@@ -85,9 +93,6 @@ def tile_picked_phpool_gelu_p_kernel(tc, x_words, x_scales, w1, w2_words, w2_sca
 
         round_w1(nc.scalar.copy, 0, 0, P, 0, 1)
         round_w1(nc.scalar.copy, 1, 0, SHARE, 0, 1)
-        w2s = keep.tile([P, BANK], U8, name="w2s", align_bytes=64)
-        nc.scalar.copy(w2s[:].bitcast(U32).rearrange("p (r n) -> p r n", n=N // 4),
-                       w2_spread[:].bitcast(U32).unsqueeze(1).to_broadcast([P, BANK // N, N // 4]))
         round_w1(nc.scalar.copy, 0, 0, P, 1, PACK)
         round_w1(nc.scalar.copy, 1, 0, SHARE, 1, PACK)
         round_w1(nc.vector.tensor_copy, 1, SHARE, P, 0, PACK)

@@ -22,7 +22,7 @@ LANES = 16
 BANK = 512
 
 LEAD = 640
-SHARE = 80
+SHARE = 40
 BYTE_PARTS = ((0, 768), (768, S))
 PIECE = 256
 CHUNK = 128
@@ -92,9 +92,8 @@ def tile_picked_phpool_gelu_p_kernel(tc, x_words, x_scales, w1, w2_words, w2_sca
             copy(w1_bf[u][:, :, m0:m1, j0:j1].rearrange("p e m j -> p m j e"), dealt[:, u, m0:m1, j0:j1])
 
         round_w1(nc.scalar.copy, 0, 0, P, 0, 1)
-        round_w1(nc.scalar.copy, 1, 0, SHARE, 0, 1)
         round_w1(nc.scalar.copy, 0, 0, P, 1, PACK)
-        round_w1(nc.scalar.copy, 1, 0, SHARE, 1, PACK)
+        round_w1(nc.scalar.copy, 1, 0, SHARE, 0, PACK)
         round_w1(nc.vector.tensor_copy, 1, SHARE, P, 0, PACK)
         for u in range(2):
             cols = slice(2 * P * u, 2 * P * (u + 1))

@@ -100,11 +100,12 @@ def tile_picked_phpool_gelu_p_kernel(tc, x_words, x_scales, w1, w2_words, w2_sca
             nc.vector.quantize_mx(out=w1_words[:, cols].bitcast(FP8X4), scales=w1_scales[:, cols], in_=w1_bf[u][:].rearrange("p e m j -> p (e m j)"))
 
         warm_bank = banks.tile([P, BANK], F32, name="bank")
-        early = (w2w[:, 0:WARM_M], w2s[:, 0:WARM_M])
-        late = (w1_words[:, 0:WARM_M], w1_scales[:, 0:WARM_M])
-        for (words, scales), n in zip([early, early, early, late, late], WARM_N):
-            nc.tensor.matmul_mx(out=warm_bank[0:WARM_M, 0:n], lhsT=words.bitcast(FP8X4), lhsT_scale=scales,
-                                rhs=w2w[:, 0:n].bitcast(FP8X4), rhs_scale=w2s[:, 0:n], start=True, stop=True)
+        def warm(bank, widths):
+            for n in widths:
+                nc.tensor.matmul_mx(out=bank[0:WARM_M, 0:n], lhsT=w2w[:, 0:WARM_M].bitcast(FP8X4), lhsT_scale=w2s[:, 0:WARM_M],
+                                    rhs=w2w[:, 0:n].bitcast(FP8X4), rhs_scale=w2s[:, 0:n], start=True, stop=True)
+
+        warm(warm_bank, WARM_N[0:3])
         nc.sync.dma_start(w2w[:, WARM_M:N].bitcast(I32), w2_rows[:, WARM_M:])
         for j in range(1, 4):
             nc.sync.dma_start(w2s[:, 0:N].bitcast(I32)[j:P:32, :], w2_scales[0].bitcast(I32)[j:16:4, :])
@@ -163,6 +164,7 @@ def tile_picked_phpool_gelu_p_kernel(tc, x_words, x_scales, w1, w2_words, w2_sca
         gelu(1, 0, CHUNK)
         both_reads(0)
         both_reads(1)
+        warm(banks.tile([P, BANK], F32, name="bank"), WARM_N[3:])
         gelu(2, 0, CHUNK)
         for h in range(2):
             for v0, v1 in LAST_PIECES[h]:

@@ -54,8 +54,8 @@ def tile_picked_phpool_gelu_p_kernel(tc, x_words, x_scales, w1, w2_words, w2_sca
         nc.sync.dma_start(w1_raw[:, 0:LEAD], w1_rows[:, 0:LEAD])
         nc.sync.dma_start(lists[:], offs)
         nc.sync.dma_start(xs[:].bitcast(I32)[0:P:8, :], x_scales[0].bitcast(I32))
-        nc.sync.dma_start(w2_spread[:].bitcast(I32), w2_scales[0].bitcast(I32).unsqueeze(1).to_broadcast([16, 8, N // 4]))
         nc.sync.dma_start(w1_raw[:, LEAD:], w1_rows[:, LEAD:])
+        nc.sync.dma_start(w2_spread[:].bitcast(I32), w2_scales[0].bitcast(I32).unsqueeze(1).to_broadcast([16, 8, N // 4]))
         xw = keep.tile([P, T], U32, name="xw", align_bytes=64)
         nc.sync.dma_start(xw[:].bitcast(I32), x_words[0].rearrange("p n t -> p (n t)").bitcast(I32))
 
@@ -78,10 +78,6 @@ def tile_picked_phpool_gelu_p_kernel(tc, x_words, x_scales, w1, w2_words, w2_sca
                 nc.sync.dma_start(placed[part][:].bitcast(I32)[j:P:32, :], picked[:].bitcast(I32)[8 * j : P : 32, :])
 
         pick_bytes(0, keep.tile([P, BYTE_PARTS[0][1]], U8, name="picked0", align_bytes=64))
-        w2s = keep.tile([P, BANK], U8, name="w2s", align_bytes=64)
-        nc.vector.tensor_copy(w2s[:].bitcast(I32).rearrange("p (r n) -> p r n", n=N // 4),
-                              w2_spread[:].bitcast(I32).unsqueeze(1).to_broadcast([P, BANK // N, N // 4]))
-        pick_bytes(1, reuse.tile([P, S - BYTE_PARTS[1][0]], U8, name="picked1", align_bytes=64, offset=0))
 
         w1_bf = [keep.tile([P, 2, P, PACK], BF16, name="w1_bf%d" % u, align_bytes=64) for u in range(2)]
         w1_words = keep.tile([P, H], U32, name="w1_words", align_bytes=64)
@@ -95,17 +91,22 @@ def tile_picked_phpool_gelu_p_kernel(tc, x_words, x_scales, w1, w2_words, w2_sca
         round_w1(nc.scalar.copy, 0, 0, P, 1, PACK)
         round_w1(nc.scalar.copy, 1, 0, SHARE, 0, PACK)
         round_w1(nc.vector.tensor_copy, 1, SHARE, P, 0, PACK)
+        w2s = keep.tile([P, BANK], U8, name="w2s", align_bytes=64)
+        nc.vector.tensor_copy(w2s[:].bitcast(I32).rearrange("p (r n) -> p r n", n=N // 4),
+                              w2_spread[:].bitcast(I32).unsqueeze(1).to_broadcast([P, BANK // N, N // 4]))
+        pick_bytes(1, reuse.tile([P, S - BYTE_PARTS[1][0]], U8, name="picked1", align_bytes=64, offset=0))
         for u in range(2):
             cols = slice(2 * P * u, 2 * P * (u + 1))
             nc.vector.quantize_mx(out=w1_words[:, cols].bitcast(FP8X4), scales=w1_scales[:, cols], in_=w1_bf[u][:].rearrange("p e m j -> p (e m j)"))
 
         warm_bank = banks.tile([P, BANK], F32, name="bank")
-        def warm(bank, widths):
+        def warm(bank, words, scales, widths):
             for n in widths:
-                nc.tensor.matmul_mx(out=bank[0:WARM_M, 0:n], lhsT=w2w[:, 0:WARM_M].bitcast(FP8X4), lhsT_scale=w2s[:, 0:WARM_M],
+                nc.tensor.matmul_mx(out=bank[0:WARM_M, 0:n], lhsT=words[:, 0:WARM_M].bitcast(FP8X4), lhsT_scale=scales[:, 0:WARM_M],
                                     rhs=w2w[:, 0:n].bitcast(FP8X4), rhs_scale=w2s[:, 0:n], start=True, stop=True)
 
-        warm(warm_bank, WARM_N[0:3])
+        warm(warm_bank, w2w, w2s, (512, 512))
+        warm(warm_bank, w1_words, w1_scales, (128, 128))
         nc.sync.dma_start(w2w[:, WARM_M:N].bitcast(I32), w2_rows[:, WARM_M:])
         for j in range(1, 4):
             nc.sync.dma_start(w2s[:, 0:N].bitcast(I32)[j:P:32, :], w2_scales[0].bitcast(I32)[j:16:4, :])
@@ -164,7 +165,7 @@ def tile_picked_phpool_gelu_p_kernel(tc, x_words, x_scales, w1, w2_words, w2_sca
         gelu(1, 0, CHUNK)
         both_reads(0)
         both_reads(1)
-        warm(banks.tile([P, BANK], F32, name="bank"), WARM_N[3:])
+        warm(banks.tile([P, BANK], F32, name="bank"), w2w, w2s, (512,))
         gelu(2, 0, CHUNK)
         for h in range(2):
             for v0, v1 in LAST_PIECES[h]:

@@ -105,8 +105,7 @@ def tile_picked_phpool_gelu_p_kernel(tc, x_words, x_scales, w1, w2_words, w2_sca
                 nc.tensor.matmul_mx(out=bank[0:WARM_M, 0:n], lhsT=words[:, 0:WARM_M].bitcast(FP8X4), lhsT_scale=scales[:, 0:WARM_M],
                                     rhs=w2w[:, 0:n].bitcast(FP8X4), rhs_scale=w2s[:, 0:n], start=True, stop=True)
 
-        warm(warm_bank, w2w, w2s, (512, 512))
-        warm(warm_bank, w1_words, w1_scales, (128, 128))
+        warm(warm_bank, w2w, w2s, (512, 512, 512))
         nc.sync.dma_start(w2w[:, WARM_M:N].bitcast(I32), w2_rows[:, WARM_M:])
         for j in range(1, 4):
             nc.sync.dma_start(w2s[:, 0:N].bitcast(I32)[j:P:32, :], w2_scales[0].bitcast(I32)[j:16:4, :])
@@ -165,7 +164,7 @@ def tile_picked_phpool_gelu_p_kernel(tc, x_words, x_scales, w1, w2_words, w2_sca
         gelu(1, 0, CHUNK)
         both_reads(0)
         both_reads(1)
-        warm(banks.tile([P, BANK], F32, name="bank"), w2w, w2s, (512,))
+        warm(banks.tile([P, BANK], F32, name="bank"), w2w, w2s, (128, 128))
         gelu(2, 0, CHUNK)
         for h in range(2):
             for v0, v1 in LAST_PIECES[h]:

@@ -130,17 +130,20 @@ def tile_picked_phpool_gelu_p_kernel(tc, x_words, x_scales, w1, w2_words, w2_sca
         last = V // CHUNK - 1
 
         def first_read(c):
-            bank = banks.tile([P, PACK, CHUNK], F32, name="bank")
-            for t in range(PACK):
-                product(bank[:, t, :], t, CHUNK * c, CHUNK)
-            first_reads[c] = keep.tile([P, CHUNK, PACK], F32, name="first_read%d" % c, align_bytes=64)
-            nc.scalar.copy(first_reads[c][:], bank[:].rearrange("p t v -> p v t"))
+            first_reads[c] = keep.tile([P, 2, CHUNK, 2], F32, name="first_read%d" % c, align_bytes=64)
+            pairs = 1 if c == 0 else 2
+            for u0 in range(0, 2, pairs):
+                bank = banks.tile([P, 2 * pairs, CHUNK], F32, name="bank")
+                for t in range(2 * pairs):
+                    product(bank[:, t, :], 2 * u0 + t, CHUNK * c, CHUNK)
+                nc.scalar.copy(first_reads[c][:, u0 : u0 + pairs], bank[:].rearrange("p (u e) v -> p u v e", e=2))
 
         def second_read(c):
             bank = banks.tile([P, PACK, CHUNK], F32, name="bank")
             for t in range(PACK):
                 product(bank[:, t, :], t, V + CHUNK * c, CHUNK)
-            nc.vector.tensor_tensor(maxima[c][:].rearrange("p (v t) -> p v t", t=PACK), bank[:].rearrange("p t v -> p v t"), first_reads[c][:], MAX)
+            nc.vector.tensor_tensor(maxima[c][:].rearrange("p (v u e) -> p v u e", u=2, e=2), bank[:].rearrange("p (u e) v -> p v u e", e=2),
+                                    first_reads[c][:].rearrange("p u v e -> p v u e"), MAX)
 
         def both_reads(h):
             bank = banks.tile([P, 2, PACK, HALF], F32, name="bank")

from contextlib import ExitStack

import concourse.mybir as mybir

K, T, S, H, N, V = 512, 2048, 1024, 512, 128, 512
FLOPS = 2 * K * H * S + 2 * H * N * V

F32 = mybir.dt.float32
BF16 = mybir.dt.bfloat16
I32 = mybir.dt.int32
U32 = mybir.dt.uint32
U16 = mybir.dt.uint16
U8 = mybir.dt.uint8
FP8X4 = mybir.dt.float8_e4m3fn_x4
GELU = mybir.ActivationFunctionType.Gelu_apprx_tanh
MAX = mybir.AluOpType.max
AXIS_X = mybir.AxisListType.X

P = 128
PACK = 4
LANES = 16
BANK = 512

LEAD = 640
SHARE = 40
BYTE_PARTS = ((0, 768), (768, S))
PIECE = 256
CHUNK = 128
HALF = 64
LAST_PIECES = (((0, 64),), ((0, 32), (32, 64)))
GROUPS = ((0, 128), (128, 256), (256, 384), (384, 448), (448, 512))
STORE = 128
GROUPS_ON_SCALAR = 2
WARM_M = 32
WARM_N = (512, 512, 512, 128, 128)


def tile_picked_phpool_gelu_p_kernel(tc, x_words, x_scales, w1, w2_words, w2_scales, offs, out):
    nc = tc.nc
    with ExitStack() as ctx:
        keep = ctx.enter_context(tc.tile_pool(name="keep", bufs=1))
        reuse = ctx.enter_context(tc.tile_pool(name="reuse", bufs=1))
        banks = ctx.enter_context(tc.psum_pool(name="banks", bufs=8))

        lists = keep.tile([P, S // LANES], U16, name="lists")
        w1_rows = w1.rearrange("(p j) c -> p (j c)", j=PACK)
        w1_raw = keep.tile([P, PACK * H], F32, name="w1_raw", align_bytes=64)
        xs = keep.tile([P, T], U8, name="xs", align_bytes=64)
        nc.vector.memset(xs[:].bitcast(I32), 0)
        w2_first = keep.tile([P, WARM_M], U32, name="w2_first", align_bytes=64)
        w2_rows = w2_words[0].rearrange("p n t -> p (n t)").bitcast(I32)
        w2_spread = reuse.tile([P, N], U8, name="w2_spread", align_bytes=64, offset=0)
        nc.scalar.dma_start(w2_first[:].bitcast(I32), w2_rows[:, 0:WARM_M])
        nc.sync.dma_start(w1_raw[:, 0:LEAD], w1_rows[:, 0:LEAD])
        nc.sync.dma_start(lists[:], offs)
        nc.sync.dma_start(xs[:].bitcast(I32)[0:P:8, :], x_scales[0].bitcast(I32))
        nc.sync.dma_start(w1_raw[:, LEAD:], w1_rows[:, LEAD:])
        nc.sync.dma_start(w2_spread[:].bitcast(I32), w2_scales[0].bitcast(I32).unsqueeze(1).to_broadcast([16, 8, N // 4]))
        xw = keep.tile([P, T], U32, name="xw", align_bytes=64)
        nc.sync.dma_start(xw[:].bitcast(I32), x_words[0].rearrange("p n t -> p (n t)").bitcast(I32))

        zero = keep.tile([P, 1], F32, name="zero")
        nc.vector.memset(zero[:], 0.0)
        bias = keep.tile([P, 1], F32, name="bias")
        nc.scalar.activation(bias[:], zero[:], GELU)
        w2w = keep.tile([P, BANK], U32, name="w2w", align_bytes=64)
        nc.scalar.copy(w2w[:].rearrange("p (r n) -> p r n", n=WARM_M), w2_first[:].unsqueeze(1).to_broadcast([P, BANK // WARM_M, WARM_M]))

        placed = []
        for part, (e0, e1) in enumerate(BYTE_PARTS):
            placed.append(keep.tile([P, e1 - e0], U8, name="placed%d" % part, align_bytes=64))
            nc.vector.memset(placed[part][:].bitcast(I32), 0)

        def pick_bytes(part, picked):
            e0, e1 = BYTE_PARTS[part]
            nc.vector.tensor_copy(picked[:], xs[:].indirect(lists[:, e0 // LANES : e1 // LANES]))
            for j in range(4):
                nc.sync.dma_start(placed[part][:].bitcast(I32)[j:P:32, :], picked[:].bitcast(I32)[8 * j : P : 32, :])

        pick_bytes(0, keep.tile([P, BYTE_PARTS[0][1]], U8, name="picked0", align_bytes=64))

        w1_bf = [keep.tile([P, 2, P, PACK], BF16, name="w1_bf%d" % u, align_bytes=64) for u in range(2)]
        w1_words = keep.tile([P, H], U32, name="w1_words", align_bytes=64)
        w1_scales = keep.tile([P, H], U8, name="w1_scales", align_bytes=64)
        dealt = w1_raw[:].rearrange("p (j m u e) -> p u m j e", j=PACK, u=2, e=2)

        def round_w1(copy, u, m0, m1, j0, j1):
            copy(w1_bf[u][:, :, m0:m1, j0:j1].rearrange("p e m j -> p m j e"), dealt[:, u, m0:m1, j0:j1])

        round_w1(nc.scalar.copy, 0, 0, P, 0, 1)
        round_w1(nc.scalar.copy, 0, 0, P, 1, PACK)
        round_w1(nc.scalar.copy, 1, 0, SHARE, 0, PACK)
        round_w1(nc.vector.tensor_copy, 1, SHARE, P, 0, PACK)
        w2s = keep.tile([P, BANK], U8, name="w2s", align_bytes=64)
        nc.vector.tensor_copy(w2s[:].bitcast(I32).rearrange("p (r n) -> p r n", n=N // 4),
                              w2_spread[:].bitcast(I32).unsqueeze(1).to_broadcast([P, BANK // N, N // 4]))
        pick_bytes(1, reuse.tile([P, S - BYTE_PARTS[1][0]], U8, name="picked1", align_bytes=64, offset=0))
        for u in range(2):
            cols = slice(2 * P * u, 2 * P * (u + 1))
            nc.vector.quantize_mx(out=w1_words[:, cols].bitcast(FP8X4), scales=w1_scales[:, cols], in_=w1_bf[u][:].rearrange("p e m j -> p (e m j)"))

        warm_bank = banks.tile([P, BANK], F32, name="bank")
        def warm(bank, words, scales, widths):
            for n in widths:
                nc.tensor.matmul_mx(out=bank[0:WARM_M, 0:n], lhsT=words[:, 0:WARM_M].bitcast(FP8X4), lhsT_scale=scales[:, 0:WARM_M],
                                    rhs=w2w[:, 0:n].bitcast(FP8X4), rhs_scale=w2s[:, 0:n], start=True, stop=True)

        warm(warm_bank, w2w, w2s, (512, 512, 512))
        nc.sync.dma_start(w2w[:, WARM_M:N].bitcast(I32), w2_rows[:, WARM_M:])
        for j in range(1, 4):
            nc.sync.dma_start(w2s[:, 0:N].bitcast(I32)[j:P:32, :], w2_scales[0].bitcast(I32)[j:16:4, :])

        pieces = {}
        for v0 in range(0, V, PIECE):
            for e0 in (v0, V + v0):
                pieces[e0 // PIECE] = keep.tile([P, PIECE], U32, name="piece%d" % (e0 // PIECE), align_bytes=64)
                nc.vector.tensor_copy(pieces[e0 // PIECE][:], xw[:].indirect(lists[:, e0 // LANES : (e0 + PIECE) // LANES]))

        def product(dst, t, e0, n):
            part = 0 if e0 < BYTE_PARTS[1][0] else 1
            s0 = e0 - BYTE_PARTS[part][0]
            nc.tensor.matmul_mx(out=dst, lhsT=w1_words[:, P * t : P * (t + 1)].bitcast(FP8X4), lhsT_scale=w1_scales[:, P * t : P * (t + 1)],
                                rhs=pieces[e0 // PIECE][:, e0 % PIECE : e0 % PIECE + n].bitcast(FP8X4), rhs_scale=placed[part][:, s0 : s0 + n],
                                start=True, stop=True)

        z = keep.tile([P, V * PACK], BF16, name="z", align_bytes=64)
        maxima = [keep.tile([P, CHUNK * PACK], F32, name="maxima%d" % c, align_bytes=64) for c in range(V // CHUNK)]
        results = [keep.tile([P, STORE], F32, name="result%d" % i, align_bytes=64) for i in range(V // STORE)]
        first_reads = {}
        last = V // CHUNK - 1

        def first_read(c):
            first_reads[c] = keep.tile([P, 2, CHUNK, 2], F32, name="first_read%d" % c, align_bytes=64)
            pairs = 1 if c == 0 else 2
            for u0 in range(0, 2, pairs):
                bank = banks.tile([P, 2 * pairs, CHUNK], F32, name="bank")
                for t in range(2 * pairs):
                    product(bank[:, t, :], 2 * u0 + t, CHUNK * c, CHUNK)
                nc.scalar.copy(first_reads[c][:, u0 : u0 + pairs], bank[:].rearrange("p (u e) v -> p u v e", e=2))

        def second_read(c):
            bank = banks.tile([P, PACK, CHUNK], F32, name="bank")
            for t in range(PACK):
                product(bank[:, t, :], t, V + CHUNK * c, CHUNK)
            nc.vector.tensor_tensor(maxima[c][:].rearrange("p (v u e) -> p v u e", u=2, e=2), bank[:].rearrange("p (u e) v -> p v u e", e=2),
                                    first_reads[c][:].rearrange("p u v e -> p v u e"), MAX)

        def both_reads(h):
            bank = banks.tile([P, 2, PACK, HALF], F32, name="bank")
            for t in range(PACK):
                for r in range(2):
                    product(bank[:, r, t, :], t, V * r + CHUNK * last + HALF * h, HALF)
            for v0, v1 in LAST_PIECES[h]:
                nc.vector.tensor_reduce(maxima[last][:, PACK * (HALF * h + v0) : PACK * (HALF * h + v1)].rearrange("p (v t) -> p v t", t=PACK),
                                        bank[:, :, :, v0:v1].rearrange("p r t v -> p v t r"), AXIS_X, MAX)

        def gelu(c, v0, v1):
            nc.scalar.activation(z[:, PACK * (CHUNK * c + v0) : PACK * (CHUNK * c + v1)], maxima[c][:, PACK * v0 : PACK * v1], GELU, bias=bias[:])

        first_read(0)
        first_read(1)
        second_read(0)
        second_read(1)
        first_read(2)
        gelu(0, 0, CHUNK)
        second_read(2)
        gelu(1, 0, CHUNK)
        both_reads(0)
        both_reads(1)
        warm(banks.tile([P, BANK], F32, name="bank"), w2w, w2s, (128, 128))
        gelu(2, 0, CHUNK)
        for h in range(2):
            for v0, v1 in LAST_PIECES[h]:
                gelu(last, HALF * h + v0, HALF * h + v1)

        sums = []
        for g, (v0, v1) in enumerate(GROUPS):
            z_words = keep.tile([P, v1 - v0], U32, name="z_words%d" % g, align_bytes=64)
            z_scales = keep.tile([P, v1 - v0], U8, name="z_scales%d" % g, align_bytes=64)
            nc.vector.quantize_mx(out=z_words[:].bitcast(FP8X4), scales=z_scales[:], in_=z[:, PACK * v0 : PACK * v1])
            sums.append(banks.tile([P, BANK], F32, name="bank"))
            nc.tensor.matmul_mx(out=sums[g][:, 0 : v1 - v0], lhsT=w2w[:, 0:N].bitcast(FP8X4), lhsT_scale=w2s[:, 0:N],
                                rhs=z_words[:].bitcast(FP8X4), rhs_scale=z_scales[:], start=True, stop=True)
        for g, (v0, v1) in enumerate(GROUPS):
            i = v0 // STORE
            copy = nc.scalar.copy if g < GROUPS_ON_SCALAR else nc.vector.tensor_copy
            copy(results[i][:, v0 - STORE * i : v1 - STORE * i], sums[g][:, 0 : v1 - v0])
            if v1 % STORE == 0:
                nc.sync.dma_start(out[:, STORE * i : STORE * (i + 1)], results[i][:])
